import numpy as np
import ml_dtypes


def mxq(x, axis, fmt="e4m3"):
    dtype, down = {"e4m3": (ml_dtypes.float8_e4m3fn, 7), "e5m2": (ml_dtypes.float8_e5m2, 14)}[fmt]
    v = np.moveaxis(np.asarray(x, np.float32).astype(ml_dtypes.bfloat16).astype(np.float64), axis, -1)
    blocks = v.reshape(v.shape[:-1] + (-1, 32))
    amax = np.abs(blocks).max(-1, keepdims=True)
    byte = np.maximum(np.where(amax > 0, np.frexp(amax)[1] - 1 + 127, 0) - down, 1)
    scale = np.exp2(byte - 127.0)
    codes = (blocks / scale).astype(np.float32).astype(dtype).astype(np.float64)
    return np.moveaxis((codes * scale).reshape(v.shape), -1, axis)


WIDE = False


def mx_kscale(k):
    if not WIDE:
        return np.ones(k)
    levels = np.array([10, -10, 5, -5, 0])
    if k % 512:
        return np.exp2(np.random.permutation(np.resize(levels, k // 32))).repeat(32)
    a = np.empty((k // 512, 16))
    for p in range(k // 512):
        a[p, :8] = np.random.permutation(np.resize(levels, 8))
        for g in range(8):
            far = levels[np.abs(levels - a[p, g]) >= 10]
            a[p, g + 8] = far[np.random.randint(len(far))]
    return np.exp2(a.ravel()).repeat(32)


def f64(x):
    return np.asarray(x).astype(np.float64)


def striped(idx):
    return np.tile(np.asarray(idx).reshape(-1, 16).T, (8, 1)).astype(np.uint16)


def unstriped(offs):
    return offs[:16].T.reshape(-1).astype(np.int64)


E2M1 = np.array([0.0, 0.5, 1.0, 1.5, 2.0, 3.0, 4.0, 6.0, -0.0, -0.5, -1.0, -1.5, -2.0, -3.0, -4.0, -6.0])


def pack_weight(w, fmt):
    k, n = w.shape
    w = f64(np.asarray(w, np.float32).astype(ml_dtypes.bfloat16)).reshape(k // 32, 32, n)
    amax = np.abs(w).max(1)
    if fmt == "e4m3":
        byte = np.frexp(amax)[1] - 1 + 127 - 7
    else:
        mant, ex = np.frexp(amax / 6.0)
        byte = np.where(mant > 0.5, ex, ex - 1) + 127
    byte = np.clip(np.where(amax > 0, byte, 1), 1, 254)
    scaled = (w * np.exp2(127.0 - byte)[:, None, :]).reshape(k, n).astype(np.float32)
    by_word = np.ascontiguousarray(scaled.reshape(k // 512, 128, 4, n).transpose(0, 1, 3, 2))
    if fmt == "e4m3":
        words = by_word.astype(ml_dtypes.float8_e4m3fn).view(np.uint8)
    else:
        c = by_word.astype(ml_dtypes.float4_e2m1fn).view(np.uint8) & 0xF
        words = (c[..., 0::2] | (c[..., 1::2] << 4)).reshape(k // 512, 128, 2 * n)
    return np.ascontiguousarray(words), np.ascontiguousarray(byte.astype(np.uint8).reshape(k // 512, 16, n))


def unpack_weight(words, scales, fmt):
    g, _, n = scales.shape
    words = np.ascontiguousarray(words).reshape(g, 128, n, -1)
    if fmt == "e4m3":
        vals = words.view(ml_dtypes.float8_e4m3fn).astype(np.float64)
    else:
        nib = np.empty((g, 128, n, 4), np.uint8)
        nib[..., 0::2] = words & 0xF
        nib[..., 1::2] = words >> 4
        vals = E2M1[nib]
    vals = vals * np.repeat(np.exp2(scales.astype(np.float64) - 127.0), 8, axis=1)[..., None]
    return vals.transpose(0, 1, 3, 2).reshape(g * 512, n)


B, N, T, D, DV, NQ = 1, 1536, 4096, 1024, 256, 128
PAGE = 512
CAP = 2.0


def setup_inputs():
    n = np.random.standard_normal
    pages = np.random.permutation(T // PAGE)[:B * N // PAGE]
    idx = (pages[:, None] * PAGE + np.arange(PAGE)[None, :]).reshape(-1)
    s = mx_kscale(D)[:, None]
    u = np.ones(T)
    u[idx] = mx_kscale(B * N)
    r = np.random.uniform(0.5, 2.0, T)
    qp = [pack_weight(x, "e4m3") for x in n((B, D, NQ)) * s * (0.80 / np.sqrt(D))]
    k = n((D, T)) / s
    v = n((DV, T)) / (u * r)
    kp = pack_weight(k, "e2m1")
    vp = pack_weight(v.T, "e4m3")
    return {
        "q_words": np.stack([x[0] for x in qp]),
        "q_scales": np.stack([x[1] for x in qp]),
        "k_words": np.ascontiguousarray(kp[0].reshape(D // 1024, 2, 128, T, 2).transpose(0, 2, 3, 1, 4)).reshape(D // 1024, 128, T, 4),
        "k_scales": kp[1],
        "v_words": vp[0],
        "v_scales": vp[1],
        "vs": np.tile(u * r, (128, 1)).astype(np.float32),
        "kb": np.tile(n(T), (128, 1)).astype(np.float32),
        "offs": striped(idx),
        "voffs": striped((pages[:, None] * DV + np.arange(DV)[None, :]).reshape(-1)),
    }


def reference(q_words, q_scales, k_words, k_scales, v_words, v_scales, vs, kb, offs, voffs):
    idx = unstriped(offs)
    k = unpack_weight(k_words.reshape(D // 1024, 128, T, 2, 2).transpose(0, 3, 1, 2, 4).reshape(D // 512, 128, 2 * T), k_scales, "e2m1")
    v = unpack_weight(v_words, v_scales, "e4m3")
    v = v.reshape(T // 512, 512, DV)[unstriped(voffs)[::DV] // DV].reshape(B, N, DV)
    pick = lambda x: x[:, idx].reshape(x.shape[0], B, N).transpose(1, 0, 2)
    q = np.stack([unpack_weight(q_words[b], q_scales[b], "e4m3") for b in range(B)])
    score = q.transpose(0, 2, 1) @ pick(k)
    score = score + pick(f64(kb))[:, :1, :]
    score = CAP * np.tanh(score / CAP)
    m = score.max(-1, keepdims=True)
    p = np.exp(score - m)
    total = p.sum(-1, keepdims=True)
    w = p * pick(f64(vs))[:, :1, :]
    y = mxq(w, 2, "e4m3") @ v
    y = y / total
    return y

@@ -1,0 +1,202 @@
+from contextlib import ExitStack
+
+import concourse.mybir as mybir
+from concourse.masks import make_identity
+
+N, T, D, DV, NQ = 1536, 4096, 1024, 256, 128
+PAGE = 512
+PAGES = N // PAGE
+POOL_PAGES = T // PAGE
+P = 128
+PASSES = D // 512
+TILES = PAGE // P
+CAP = 2.0
+KB_ROW = 16
+
+FLOPS = 2 * NQ * N * (D + DV)
+
+F32 = mybir.dt.float32
+BF16 = mybir.dt.bfloat16
+I32 = mybir.dt.int32
+U32 = mybir.dt.uint32
+U16 = mybir.dt.uint16
+U8 = mybir.dt.uint8
+FP8X4 = mybir.dt.float8_e4m3fn_x4
+FP4X4 = mybir.dt.float4_e2m1fn_x4
+ACT = mybir.ActivationFunctionType
+ALU = mybir.AluOpType
+AX = mybir.AxisListType
+
+
+def tile_attend_pkv4q_soft_cap_kb_kernel(
+    tc, q_words, q_scales, k_words, k_scales, v_words, v_scales, vs, kb, offs, voffs, out
+):
+    nc = tc.nc
+    with ExitStack() as ctx:
+        sb = ctx.enter_context(tc.tile_pool(name="sb", bufs=1))
+        ps = ctx.enter_context(tc.psum_pool(name="ps", bufs=1))
+
+        def tile(name, shape, dtype, tag=None):
+            return sb.tile(shape, dtype, name=name, tag=tag or name, align_bytes=64)
+
+        offsets = sb.tile([P, N // 16], U16, name="offsets")
+        voffsets = sb.tile([P, PAGES * DV // 16], U16, name="voffsets")
+        kw_pool = tile("kw_pool", [P, T], I32)
+        ks_pool = tile("ks_pool", [P, T], U8)
+        kb_pool = tile("kb_pool", [P, T], F32)
+        vs_pool = tile("vs_pool", [P, T], F32)
+        vw_pool = tile("vw_pool", [P, POOL_PAGES * DV], I32)
+        vsc_pool = tile("vsc_pool", [P, POOL_PAGES * DV], U8)
+        qw = tile("qw", [P, PASSES, NQ], I32)
+        qs = tile("qs", [P, PASSES, NQ], U8)
+        ks_rows = tile("ks_rows", [P, N], U8)
+        ks_plane = tile("ks_plane", [P, N], U8)
+        ident = tile("ident", [P, P], F32)
+        warm = tile("warm", [P, 1], F32)
+
+        def page_offsets(e):
+            return offsets[:, e * PAGE // 16 : (e + 1) * PAGE // 16]
+
+        ks_flat = k_scales.rearrange("o f t -> (o f) t").bitcast(I32)
+        nc.sync.dma_start(offsets[:], offs)
+        nc.sync.dma_start(kw_pool[:], k_words[0].rearrange("g t b -> g (t b)").bitcast(I32))
+        nc.vector.memset(ks_pool[:].bitcast(I32), 0)
+        for quad in (1, 2, 3):
+            nc.scalar.dma_start(ks_pool[32 * quad : 32 * quad + 4, :].bitcast(I32), ks_flat[4 * quad : 4 * quad + 4, :])
+        nc.scalar.dma_start(ks_pool[0:32, :].bitcast(I32), ks_flat)
+        nc.vector.memset(kb_pool[:], 0.0)
+        nc.scalar.dma_start(kb_pool[KB_ROW : KB_ROW + 1, :], kb[0:1, :])
+        nc.vector.memset(warm[:], 0.0)
+        nc.scalar.activation(warm[:], warm[:], ACT.Exp)
+        nc.sync.dma_start(qw[:], q_words[0].rearrange("o g q r -> g o (q r)").bitcast(I32))
+        nc.sync.dma_start(
+            vw_pool[:].rearrange("g (u e) -> g u e", u=POOL_PAGES),
+            v_words.rearrange("u g e r -> g u (e r)").bitcast(I32),
+        )
+        nc.sync.dma_start(voffsets[:], voffs)
+        nc.sync.dma_start(vs_pool[:], vs)
+        nc.gpsimd.memset(qs[:].bitcast(I32), 0)
+        for quad in range(4):
+            nc.gpsimd.dma_start(
+                qs[32 * quad : 32 * quad + 4, :, :].bitcast(I32),
+                q_scales[0, :, 4 * quad : 4 * quad + 4, :].rearrange("o r q -> r o q").bitcast(I32),
+            )
+        make_identity(nc, ident[:])
+        nc.vector.memset(ks_plane[:].bitcast(I32), 0)
+        nc.vector.memset(vsc_pool[:].bitcast(I32), 0)
+        for quad in range(4):
+            nc.gpsimd.dma_start(
+                vsc_pool[32 * quad : 32 * quad + 4, :].rearrange("r (u e) -> r u e", u=POOL_PAGES).bitcast(I32),
+                v_scales[:, 4 * quad : 4 * quad + 4, :].rearrange("u r e -> r u e").bitcast(I32),
+            )
+
+        nc.vector.tensor_copy(ks_rows[:], ks_pool[:].indirect(offsets[:]))
+        for quad in range(4):
+            nc.scalar.dma_start(
+                ks_plane[32 * quad : 32 * quad + 4, :].bitcast(I32),
+                ks_rows[16 + 4 * quad : 20 + 4 * quad, :].bitcast(I32),
+            )
+        key_planes = (ks_rows, ks_plane)
+
+        half_kb = tile("half_kb", [P, PAGES * TILES], F32)
+        for e in range(PAGES):
+            kb_g = tile("kb_g%d" % e, [P, PAGE], F32)
+            nc.vector.tensor_copy(kb_g[:], kb_pool[:].indirect(page_offsets(e)))
+            kb_t = ps.tile([P, TILES, P], F32, name="kb_t%d" % e, tag="turn%d" % e)
+            for j in range(TILES):
+                nc.tensor.transpose(kb_t[:, j, :], kb_g[:, j * P : (j + 1) * P], ident[:])
+            nc.scalar.mul(half_kb[:, e * TILES : (e + 1) * TILES], kb_t[:, :, KB_ROW], 1.0 / CAP)
+
+        expc = []
+        sums = tile("sums", [P, PAGES], F32)
+        for e in range(PAGES):
+            kw_g = tile("kw_g%d" % e, [P, PAGE], U32, tag="kb_pool" if e == 0 else None)
+            nc.vector.tensor_copy(kw_g[:], kw_pool[:].bitcast(U32).indirect(page_offsets(e)))
+            k4 = tile("k4_%d" % e, [P, PASSES, 2 * PAGE], U8)
+            nc.vector.tensor_copy(k4[:].bitcast(U16), kw_g[:].bitcast(U16).rearrange("g (n o) -> g o n", o=PASSES))
+            s_t = ps.tile([P, TILES, NQ], F32, name="s_t%d" % e, tag="score%d" % e)
+            for j in range(TILES):
+                for o in range(PASSES):
+                    nc.tensor.matmul_mx(
+                        out=s_t[:, j, :],
+                        lhsT=k4[:, o, 2 * j * P : 2 * (j + 1) * P].bitcast(FP4X4),
+                        lhsT_scale=key_planes[o][:, e * PAGE + j * P : e * PAGE + (j + 1) * P],
+                        rhs=qw[:, o, :].bitcast(FP8X4),
+                        rhs_scale=qs[:, o, :],
+                        start=(o == 0),
+                        stop=(o == PASSES - 1),
+                    )
+            th_t = tile("th_t%d" % e, [P, TILES, NQ], F32)
+            for j in range(TILES):
+                col = e * TILES + j
+                nc.scalar.activation(
+                    th_t[:, j, :], s_t[:, j, :], ACT.Tanh, bias=half_kb[:, col : col + 1], scale=1.0 / CAP
+                )
+            th = ps.tile([P, TILES, P], F32, name="th%d" % e, tag="turn%d" % e)
+            for j in range(TILES):
+                nc.tensor.transpose(th[:, j, :], th_t[:, j, :], ident[:])
+            ex = tile("ex%d" % e, [P, PAGE], F32)
+            nc.scalar.activation(
+                ex[:], th[:].rearrange("q j k -> q (j k)"), ACT.Exp, scale=CAP, accum_out=sums[:, e : e + 1]
+            )
+            expc.append(ex)
+
+        vw_g = tile("vw_g", [P, PAGES * DV], U32, tag="kw_pool")
+        vsc_g = tile("vsc_g", [P, PAGES * DV], U8, tag="kw_g%d" % (PAGES - 1))
+        nc.vector.tensor_copy(vw_g[:], vw_pool[:].bitcast(U32).indirect(voffsets[:]))
+        nc.vector.tensor_copy(vsc_g[:], vsc_pool[:].indirect(voffsets[:]))
+        tops = tile("tops", [P, PAGES], F32)
+        top = tile("top", [P, 1], F32)
+        inv_top = tile("inv_top", [P, 1], F32)
+        scaled = []
+        for e in range(PAGES):
+            nc.vector.tensor_reduce(tops[:, e : e + 1], expc[e][:], AX.X, ALU.max)
+        nc.vector.tensor_reduce(top[:], tops[:], AX.X, ALU.max)
+        w0_all = tile("w0", [P, PAGES, PAGE], F32, tag="tops")
+        for e in range(PAGES):
+            w0 = w0_all[:, e, :]
+            nc.vector.tensor_tensor(w0, vs_pool[:].indirect(page_offsets(e)), expc[e][:], ALU.mult)
+            if e == 0:
+                nc.vector.reciprocal(inv_top[:], top[:])
+            scaled.append(w0)
+
+        total = tile("total", [P, 1], F32)
+        inv_total = tile("inv_total", [P, 1], F32)
+        factor = tile("factor", [P, 1], F32)
+
+        acc = ps.tile([P, DV], F32, name="acc", tag="acc")
+        for e in range(PAGES):
+            wb = tile("wb%d" % e, [P, 2, P, 2], BF16)
+            source = scaled[e].rearrange("q (g u c) -> q u g c", u=2, c=2)
+            if e < PAGES - 1:
+                nc.scalar.activation(wb[:], source, ACT.Copy, scale=inv_top[:])
+            else:
+                nc.vector.tensor_scalar_mul(wb[:], source, inv_top[:])
+            words = wb[:].rearrange("q u g c -> q (u g c)").bitcast(F32)
+            w_t = ps.tile([P, 2, NQ], F32, name="w_t%d" % e, tag="score%d" % e)
+            for u in range(2):
+                nc.tensor.transpose(w_t[:, u, :], words[:, u * P : (u + 1) * P], ident[:])
+            wq = tile("wq%d" % e, [P, 4 * NQ], BF16)
+            nc.scalar.copy(
+                wq[:].bitcast(F32).rearrange("g (q u) -> g q u", u=2), w_t[:].rearrange("g u q -> g q u")
+            )
+            codes = tile("codes%d" % e, [P, NQ], U32)
+            scales = tile("scales%d" % e, [P, NQ], U8)
+            nc.vector.quantize_mx(out=codes[:].bitcast(FP8X4), scales=scales[:], in_=wq[:])
+            nc.tensor.matmul_mx(
+                out=acc[:],
+                lhsT=codes[:].bitcast(FP8X4),
+                lhsT_scale=scales[:],
+                rhs=vw_g[:, e * DV : (e + 1) * DV].bitcast(FP8X4),
+                rhs_scale=vsc_g[:, e * DV : (e + 1) * DV],
+                start=(e == 0),
+                stop=(e == PAGES - 1),
+            )
+            if e == 0:
+                nc.vector.tensor_reduce(total[:], sums[:], AX.X, ALU.add)
+                nc.vector.reciprocal(inv_total[:], total[:])
+                nc.vector.tensor_tensor(factor[:], inv_total[:], top[:], ALU.mult)
+
+        result = tile("result", [P, DV], F32)
+        nc.scalar.activation(result[:], acc[:], ACT.Copy, scale=factor[:])
+        nc.sync.dma_start(out[0], result[:])

@@ -58,45 +58,54 @@ def tile_attend_pkv4q_soft_cap_kb_kernel(
             return offsets[:, e * PAGE // 16 : (e + 1) * PAGE // 16]
 
         ks_flat = k_scales.rearrange("o f t -> (o f) t").bitcast(I32)
-        nc.sync.dma_start(offsets[:], offs)
-        nc.sync.dma_start(kw_pool[:], k_words[0].rearrange("g t b -> g (t b)").bitcast(I32))
-        nc.vector.memset(ks_pool[:].bitcast(I32), 0)
-        for quad in (1, 2, 3):
-            nc.scalar.dma_start(ks_pool[32 * quad : 32 * quad + 4, :].bitcast(I32), ks_flat[4 * quad : 4 * quad + 4, :])
-        nc.scalar.dma_start(ks_pool[0:32, :].bitcast(I32), ks_flat)
-        nc.vector.memset(kb_pool[:], 0.0)
-        nc.scalar.dma_start(kb_pool[KB_ROW : KB_ROW + 1, :], kb[0:1, :])
-        nc.vector.memset(warm[:], 0.0)
-        nc.scalar.activation(warm[:], warm[:], ACT.Exp)
-        nc.sync.dma_start(qw[:], q_words[0].rearrange("o g q r -> g o (q r)").bitcast(I32))
-        nc.sync.dma_start(
-            vw_pool[:].rearrange("g (u e) -> g u e", u=POOL_PAGES),
-            v_words.rearrange("u g e r -> g u (e r)").bitcast(I32),
-        )
-        nc.sync.dma_start(voffsets[:], voffs)
-        nc.sync.dma_start(vs_pool[:], vs)
-        nc.gpsimd.memset(qs[:].bitcast(I32), 0)
-        for quad in range(4):
-            nc.gpsimd.dma_start(
+        kw_flat = k_words[0].rearrange("g t b -> g (t b)").bitcast(I32)
+
+        def load_q_scales(quad):
+            nc.sync.dma_start(
                 qs[32 * quad : 32 * quad + 4, :, :].bitcast(I32),
                 q_scales[0, :, 4 * quad : 4 * quad + 4, :].rearrange("o r q -> r o q").bitcast(I32),
             )
-        make_identity(nc, ident[:])
+
+        nc.vector.memset(qs[:].bitcast(I32), 0)
+        nc.vector.memset(ks_pool[:].bitcast(I32), 0)
+        nc.vector.memset(warm[:], 0.0)
+        nc.vector.memset(kb_pool[:], 0.0)
         nc.vector.memset(ks_plane[:].bitcast(I32), 0)
         nc.vector.memset(vsc_pool[:].bitcast(I32), 0)
-        for quad in range(4):
-            nc.gpsimd.dma_start(
-                vsc_pool[32 * quad : 32 * quad + 4, :].rearrange("r (u e) -> r u e", u=POOL_PAGES).bitcast(I32),
-                v_scales[:, 4 * quad : 4 * quad + 4, :].rearrange("u r e -> r u e").bitcast(I32),
-            )
+        nc.scalar.activation(warm[:], warm[:], ACT.Exp)
+        make_identity(nc, ident[:])
+
+        nc.sync.dma_start(offsets[:], offs)
+        nc.sync.dma_start(qw[:], q_words[0].rearrange("o g q r -> g o (q r)").bitcast(I32))
+        load_q_scales(0)
+        nc.sync.dma_start(ks_pool[0:32, :].bitcast(I32), ks_flat)
+        for quad in (1, 2, 3):
+            nc.sync.dma_start(ks_pool[32 * quad : 32 * quad + 4, :].bitcast(I32), ks_flat[4 * quad : 4 * quad + 4, :])
+        nc.sync.dma_start(kw_pool[:, : T // 2], kw_flat[:, : T // 2])
+        nc.sync.dma_start(kb_pool[KB_ROW : KB_ROW + 1, :], kb[0:1, :])
+        for quad in (1, 2, 3):
+            load_q_scales(quad)
+        nc.sync.dma_start(kw_pool[:, T // 2 :], kw_flat[:, T // 2 :])
 
         nc.vector.tensor_copy(ks_rows[:], ks_pool[:].indirect(offsets[:]))
         for quad in range(4):
-            nc.scalar.dma_start(
+            nc.sync.dma_start(
                 ks_plane[32 * quad : 32 * quad + 4, :].bitcast(I32),
                 ks_rows[16 + 4 * quad : 20 + 4 * quad, :].bitcast(I32),
             )
         key_planes = (ks_rows, ks_plane)
+
+        nc.sync.dma_start(voffsets[:], voffs)
+        nc.sync.dma_start(
+            vw_pool[:].rearrange("g (u e) -> g u e", u=POOL_PAGES),
+            v_words.rearrange("u g e r -> g u (e r)").bitcast(I32),
+        )
+        for quad in range(4):
+            nc.sync.dma_start(
+                vsc_pool[32 * quad : 32 * quad + 4, :].rearrange("r (u e) -> r u e", u=POOL_PAGES).bitcast(I32),
+                v_scales[:, 4 * quad : 4 * quad + 4, :].rearrange("u r e -> r u e").bitcast(I32),
+            )
+        nc.sync.dma_start(vs_pool[:], vs)
 
         half_kb = tile("half_kb", [P, PAGES * TILES], F32)
         for e in range(PAGES):
@@ -110,7 +119,7 @@ def tile_attend_pkv4q_soft_cap_kb_kernel(
         expc = []
         sums = tile("sums", [P, PAGES], F32)
         for e in range(PAGES):
-            kw_g = tile("kw_g%d" % e, [P, PAGE], U32, tag="kb_pool" if e == 0 else None)
+            kw_g = tile("kw_g%d" % e, [P, PAGE], U32)
             nc.vector.tensor_copy(kw_g[:], kw_pool[:].bitcast(U32).indirect(page_offsets(e)))
             k4 = tile("k4_%d" % e, [P, PASSES, 2 * PAGE], U8)
             nc.vector.tensor_copy(k4[:].bitcast(U16), kw_g[:].bitcast(U16).rearrange("g (n o) -> g o n", o=PASSES))

@@ -11,7 +11,7 @@ P = 128
 PASSES = D // 512
 TILES = PAGE // P
 CAP = 2.0
-KB_ROW = 16
+KB_ROW = P - 1
 
 FLOPS = 2 * NQ * N * (D + DV)
 
@@ -66,24 +66,25 @@ def tile_attend_pkv4q_soft_cap_kb_kernel(
                 q_scales[0, :, 4 * quad : 4 * quad + 4, :].rearrange("o r q -> r o q").bitcast(I32),
             )
 
-        nc.vector.memset(qs[:].bitcast(I32), 0)
         nc.vector.memset(ks_pool[:].bitcast(I32), 0)
         nc.vector.memset(warm[:], 0.0)
-        nc.vector.memset(kb_pool[:], 0.0)
+        nc.vector.memset(qs[:].bitcast(I32), 0)
+        nc.vector.memset(kb_pool[:KB_ROW, :], 0.0)
         nc.vector.memset(ks_plane[:].bitcast(I32), 0)
         nc.vector.memset(vsc_pool[:].bitcast(I32), 0)
         nc.scalar.activation(warm[:], warm[:], ACT.Exp)
         make_identity(nc, ident[:])
 
+        vs_rows = tile("vs_rows", [P, T // P], F32)
         nc.sync.dma_start(offsets[:], offs)
-        nc.sync.dma_start(qw[:], q_words[0].rearrange("o g q r -> g o (q r)").bitcast(I32))
-        load_q_scales(0)
         nc.sync.dma_start(ks_pool[0:32, :].bitcast(I32), ks_flat)
         for quad in (1, 2, 3):
             nc.sync.dma_start(ks_pool[32 * quad : 32 * quad + 4, :].bitcast(I32), ks_flat[4 * quad : 4 * quad + 4, :])
-        nc.sync.dma_start(kw_pool[:, : T // 2], kw_flat[:, : T // 2])
+        nc.sync.dma_start(vs_rows[:], vs[0].rearrange("(p c) -> p c", p=P))
         nc.sync.dma_start(kb_pool[KB_ROW : KB_ROW + 1, :], kb[0:1, :])
-        for quad in (1, 2, 3):
+        nc.sync.dma_start(kw_pool[:, : T // 2], kw_flat[:, : T // 2])
+        nc.sync.dma_start(qw[:], q_words[0].rearrange("o g q r -> g o (q r)").bitcast(I32))
+        for quad in range(4):
             load_q_scales(quad)
         nc.sync.dma_start(kw_pool[:, T // 2 :], kw_flat[:, T // 2 :])
 
@@ -105,7 +106,14 @@ def tile_attend_pkv4q_soft_cap_kb_kernel(
                 vsc_pool[32 * quad : 32 * quad + 4, :].rearrange("r (u e) -> r u e", u=POOL_PAGES).bitcast(I32),
                 v_scales[:, 4 * quad : 4 * quad + 4, :].rearrange("u r e -> r u e").bitcast(I32),
             )
-        nc.sync.dma_start(vs_pool[:], vs)
+
+        vs_view = vs_pool[:].rearrange("m (n c) -> m n c", c=T // P)
+        for blk in range(T // P // TILES):
+            spread = ps.tile([P, TILES, P], F32, name="spread%d" % blk, tag="score%d" % (blk % PAGES))
+            for j in range(TILES):
+                c = blk * TILES + j
+                nc.tensor.transpose(spread[:, j, :], vs_rows[:, c : c + 1].to_broadcast([P, P]), ident[:])
+            nc.scalar.copy(vs_view[:, :, blk * TILES : (blk + 1) * TILES], spread[:].rearrange("m j n -> m n j"))
 
         half_kb = tile("half_kb", [P, PAGES * TILES], F32)
         for e in range(PAGES):

@@ -12,6 +12,9 @@ PASSES = D // 512
 TILES = PAGE // P
 CAP = 2.0
 KB_ROW = P - 1
+HALF = PAGE // 2
+HALVES = N // HALF
+SCORE_BANKS = 3
 
 FLOPS = 2 * NQ * N * (D + DV)
 
@@ -52,7 +55,12 @@ def tile_attend_pkv4q_soft_cap_kb_kernel(
         ks_rows = tile("ks_rows", [P, N], U8)
         ks_plane = tile("ks_plane", [P, N], U8)
         ident = tile("ident", [P, P], F32)
-        warm = tile("warm", [P, 1], F32)
+
+        expc = [tile("ex%d" % h, [P, HALF + (2 if h == HALVES - 1 else 0)], F32) for h in range(HALVES)]
+        floor = expc[-1][:, HALF + 1 :]
+
+        def half_offsets(h):
+            return offsets[:, h * HALF // 16 : (h + 1) * HALF // 16]
 
         def page_offsets(e):
             return offsets[:, e * PAGE // 16 : (e + 1) * PAGE // 16]
@@ -67,12 +75,12 @@ def tile_attend_pkv4q_soft_cap_kb_kernel(
             )
 
         nc.vector.memset(ks_pool[:].bitcast(I32), 0)
-        nc.vector.memset(warm[:], 0.0)
+        nc.vector.memset(floor, -CAP)
         nc.vector.memset(qs[:].bitcast(I32), 0)
-        nc.vector.memset(kb_pool[:KB_ROW, :], 0.0)
+        nc.vector.memset(kb_pool[:KB_ROW, :].bitcast(I32), 0)
         nc.vector.memset(ks_plane[:].bitcast(I32), 0)
         nc.vector.memset(vsc_pool[:].bitcast(I32), 0)
-        nc.scalar.activation(warm[:], warm[:], ACT.Exp)
+        nc.scalar.activation(floor, floor, ACT.Exp)
         make_identity(nc, ident[:])
 
         vs_rows = tile("vs_rows", [P, T // P], F32)
@@ -97,15 +105,15 @@ def tile_attend_pkv4q_soft_cap_kb_kernel(
         key_planes = (ks_rows, ks_plane)
 
         nc.sync.dma_start(voffsets[:], voffs)
-        nc.sync.dma_start(
-            vw_pool[:].rearrange("g (u e) -> g u e", u=POOL_PAGES),
-            v_words.rearrange("u g e r -> g u (e r)").bitcast(I32),
-        )
         for quad in range(4):
             nc.sync.dma_start(
                 vsc_pool[32 * quad : 32 * quad + 4, :].rearrange("r (u e) -> r u e", u=POOL_PAGES).bitcast(I32),
                 v_scales[:, 4 * quad : 4 * quad + 4, :].rearrange("u r e -> r u e").bitcast(I32),
             )
+        nc.sync.dma_start(
+            vw_pool[:].rearrange("g (u e) -> g u e", u=POOL_PAGES),
+            v_words.rearrange("u g e r -> g u (e r)").bitcast(I32),
+        )
 
         vs_view = vs_pool[:].rearrange("m (n c) -> m n c", c=T // P)
         for blk in range(T // P // TILES):
@@ -124,72 +132,91 @@ def tile_attend_pkv4q_soft_cap_kb_kernel(
                 nc.tensor.transpose(kb_t[:, j, :], kb_g[:, j * P : (j + 1) * P], ident[:])
             nc.scalar.mul(half_kb[:, e * TILES : (e + 1) * TILES], kb_t[:, :, KB_ROW], 1.0 / CAP)
 
-        expc = []
-        sums = tile("sums", [P, PAGES], F32)
-        for e in range(PAGES):
-            kw_g = tile("kw_g%d" % e, [P, PAGE], U32)
-            nc.vector.tensor_copy(kw_g[:], kw_pool[:].bitcast(U32).indirect(page_offsets(e)))
-            k4 = tile("k4_%d" % e, [P, PASSES, 2 * PAGE], U8)
-            nc.vector.tensor_copy(k4[:].bitcast(U16), kw_g[:].bitcast(U16).rearrange("g (n o) -> g o n", o=PASSES))
-            s_t = ps.tile([P, TILES, NQ], F32, name="s_t%d" % e, tag="score%d" % e)
-            for j in range(TILES):
+        sums = tile("sums", [P, HALVES], F32)
+        kw_g = [tile("kw_g%d" % e, [P, PAGE], U32) for e in range(PAGES)]
+        k4 = [tile("k4_%d" % h, [P, PASSES, 2 * HALF], U8) for h in range(HALVES)]
+
+        def gather_keys(e):
+            nc.vector.tensor_copy(kw_g[e][:], kw_pool[:].bitcast(U32).indirect(page_offsets(e)))
+
+        def part_keys(h):
+            words = kw_g[h // 2][:, h % 2 * HALF : (h % 2 + 1) * HALF]
+            nc.vector.tensor_copy(k4[h][:].bitcast(U16), words.bitcast(U16).rearrange("g (n o) -> g o n", o=PASSES))
+
+        gather_keys(0)
+        for h in range(HALVES):
+            part_keys(h)
+            if h % 2 == 0 and h // 2 + 1 < PAGES:
+                gather_keys(h // 2 + 1)
+
+        for h in range(HALVES):
+            s_t = ps.tile([P, 2, NQ], F32, name="s_t%d" % h, tag="score%d" % (h % SCORE_BANKS))
+            for j in range(2):
                 for o in range(PASSES):
                     nc.tensor.matmul_mx(
                         out=s_t[:, j, :],
-                        lhsT=k4[:, o, 2 * j * P : 2 * (j + 1) * P].bitcast(FP4X4),
-                        lhsT_scale=key_planes[o][:, e * PAGE + j * P : e * PAGE + (j + 1) * P],
+                        lhsT=k4[h][:, o, 2 * j * P : 2 * (j + 1) * P].bitcast(FP4X4),
+                        lhsT_scale=key_planes[o][:, h * HALF + j * P : h * HALF + (j + 1) * P],
                         rhs=qw[:, o, :].bitcast(FP8X4),
                         rhs_scale=qs[:, o, :],
                         start=(o == 0),
                         stop=(o == PASSES - 1),
                     )
-            th_t = tile("th_t%d" % e, [P, TILES, NQ], F32)
-            for j in range(TILES):
-                col = e * TILES + j
+            th_t = tile("th_t%d" % h, [P, 2, NQ], F32)
+            for j in range(2):
+                col = 2 * h + j
                 nc.scalar.activation(
                     th_t[:, j, :], s_t[:, j, :], ACT.Tanh, bias=half_kb[:, col : col + 1], scale=1.0 / CAP
                 )
-            th = ps.tile([P, TILES, P], F32, name="th%d" % e, tag="turn%d" % e)
-            for j in range(TILES):
+            th = ps.tile([P, 2, P], F32, name="th%d" % h, tag="turn%d" % (h % PAGES))
+            for j in range(2):
                 nc.tensor.transpose(th[:, j, :], th_t[:, j, :], ident[:])
-            ex = tile("ex%d" % e, [P, PAGE], F32)
             nc.scalar.activation(
-                ex[:], th[:].rearrange("q j k -> q (j k)"), ACT.Exp, scale=CAP, accum_out=sums[:, e : e + 1]
+                expc[h][:, :HALF], th[:].rearrange("q j k -> q (j k)"), ACT.Exp, scale=CAP, accum_out=sums[:, h : h + 1]
             )
-            expc.append(ex)
 
-        vw_g = tile("vw_g", [P, PAGES * DV], U32, tag="kw_pool")
         vsc_g = tile("vsc_g", [P, PAGES * DV], U8, tag="kw_g%d" % (PAGES - 1))
-        nc.vector.tensor_copy(vw_g[:], vw_pool[:].bitcast(U32).indirect(voffsets[:]))
         nc.vector.tensor_copy(vsc_g[:], vsc_pool[:].indirect(voffsets[:]))
-        tops = tile("tops", [P, PAGES], F32)
+        products = tile("products", [P, N + HALVES], F32, tag="vsc_pool")
+        tops = products[:, N : N + HALVES - 1]
+        total = products[:, N + HALVES - 1 :]
         top = tile("top", [P, 1], F32)
         inv_top = tile("inv_top", [P, 1], F32)
-        scaled = []
-        for e in range(PAGES):
-            nc.vector.tensor_reduce(tops[:, e : e + 1], expc[e][:], AX.X, ALU.max)
-        nc.vector.tensor_reduce(top[:], tops[:], AX.X, ALU.max)
-        w0_all = tile("w0", [P, PAGES, PAGE], F32, tag="tops")
-        for e in range(PAGES):
-            w0 = w0_all[:, e, :]
-            nc.vector.tensor_tensor(w0, vs_pool[:].indirect(page_offsets(e)), expc[e][:], ALU.mult)
-            if e == 0:
+        scaled = [products[:, e * PAGE : (e + 1) * PAGE] for e in range(PAGES)]
+        for h in range(HALVES):
+            if h < HALVES - 1:
+                nc.vector.tensor_reduce(tops[:, h : h + 1], expc[h][:], AX.X, ALU.max)
+            else:
+                nc.vector.tensor_reduce(top[:], expc[h][:], AX.X, ALU.max)
                 nc.vector.reciprocal(inv_top[:], top[:])
-            scaled.append(w0)
+            w0 = scaled[h // 2][:, h % 2 * HALF : (h % 2 + 1) * HALF]
+            nc.vector.tensor_tensor(w0, vs_pool[:].indirect(half_offsets(h)), expc[h][:, :HALF], ALU.mult)
+            if h == HALVES - 2:
+                nc.vector.tensor_reduce(expc[-1][:, HALF : HALF + 1], tops, AX.X, ALU.max)
 
-        total = tile("total", [P, 1], F32)
-        inv_total = tile("inv_total", [P, 1], F32)
+        ratio = tile("ratio", [P, 1], F32)
         factor = tile("factor", [P, 1], F32)
 
-        acc = ps.tile([P, DV], F32, name="acc", tag="acc")
+        rounded = []
         for e in range(PAGES):
             wb = tile("wb%d" % e, [P, 2, P, 2], BF16)
             source = scaled[e].rearrange("q (g u c) -> q u g c", u=2, c=2)
-            if e < PAGES - 1:
+            if e == 0:
                 nc.scalar.activation(wb[:], source, ACT.Copy, scale=inv_top[:])
             else:
                 nc.vector.tensor_scalar_mul(wb[:], source, inv_top[:])
-            words = wb[:].rearrange("q u g c -> q (u g c)").bitcast(F32)
+            rounded.append(wb)
+
+        nc.vector.tensor_reduce(total, sums[:], AX.X, ALU.add)
+        nc.vector.tensor_tensor(ratio[:], total, inv_top[:], ALU.mult)
+        nc.vector.reciprocal(factor[:], ratio[:])
+
+        vw_g = tile("vw_g", [P, PAGES * DV], U32, tag="vsc_pool")
+        nc.vector.tensor_copy(vw_g[:], vw_pool[:].bitcast(U32).indirect(voffsets[:]))
+
+        acc = ps.tile([P, DV], F32, name="acc", tag="acc")
+        for e in range(PAGES):
+            words = rounded[e][:].rearrange("q u g c -> q (u g c)").bitcast(F32)
             w_t = ps.tile([P, 2, NQ], F32, name="w_t%d" % e, tag="score%d" % e)
             for u in range(2):
                 nc.tensor.transpose(w_t[:, u, :], words[:, u * P : (u + 1) * P], ident[:])
@@ -209,10 +236,6 @@ def tile_attend_pkv4q_soft_cap_kb_kernel(
                 start=(e == 0),
                 stop=(e == PAGES - 1),
             )
-            if e == 0:
-                nc.vector.tensor_reduce(total[:], sums[:], AX.X, ALU.add)
-                nc.vector.reciprocal(inv_total[:], total[:])
-                nc.vector.tensor_tensor(factor[:], inv_total[:], top[:], ALU.mult)
 
         result = tile("result", [P, DV], F32)
         nc.scalar.activation(result[:], acc[:], ACT.Copy, scale=factor[:])

@@ -15,6 +15,8 @@ KB_ROW = P - 1
 HALF = PAGE // 2
 HALVES = N // HALF
 SCORE_BANKS = 3
+KW_CUTS = (0, T // 2, T)
+SPREAD = T // 2
 
 FLOPS = 2 * NQ * N * (D + DV)
 
@@ -80,21 +82,25 @@ def tile_attend_pkv4q_soft_cap_kb_kernel(
         nc.vector.memset(kb_pool[:KB_ROW, :].bitcast(I32), 0)
         nc.vector.memset(ks_plane[:].bitcast(I32), 0)
         nc.vector.memset(vsc_pool[:].bitcast(I32), 0)
-        nc.scalar.activation(floor, floor, ACT.Exp)
         make_identity(nc, ident[:])
+        nc.scalar.activation(floor, floor, ACT.Exp)
 
-        vs_rows = tile("vs_rows", [P, T // P], F32)
+        def load_key_words(piece):
+            cols = slice(KW_CUTS[piece], KW_CUTS[piece + 1])
+            nc.sync.dma_start(kw_pool[:, cols], kw_flat[:, cols])
+
+        vs_rows = tile("vs_rows", [P, SPREAD // P], F32)
         nc.sync.dma_start(offsets[:], offs)
+        nc.sync.dma_start(vs_rows[:], vs[0, :SPREAD].rearrange("(p c) -> p c", p=P))
         nc.sync.dma_start(ks_pool[0:32, :].bitcast(I32), ks_flat)
         for quad in (1, 2, 3):
             nc.sync.dma_start(ks_pool[32 * quad : 32 * quad + 4, :].bitcast(I32), ks_flat[4 * quad : 4 * quad + 4, :])
-        nc.sync.dma_start(vs_rows[:], vs[0].rearrange("(p c) -> p c", p=P))
         nc.sync.dma_start(kb_pool[KB_ROW : KB_ROW + 1, :], kb[0:1, :])
-        nc.sync.dma_start(kw_pool[:, : T // 2], kw_flat[:, : T // 2])
+        load_key_words(0)
         nc.sync.dma_start(qw[:], q_words[0].rearrange("o g q r -> g o (q r)").bitcast(I32))
         for quad in range(4):
             load_q_scales(quad)
-        nc.sync.dma_start(kw_pool[:, T // 2 :], kw_flat[:, T // 2 :])
+        load_key_words(1)
 
         nc.vector.tensor_copy(ks_rows[:], ks_pool[:].indirect(offsets[:]))
         for quad in range(4):
@@ -103,20 +109,20 @@ def tile_attend_pkv4q_soft_cap_kb_kernel(
                 ks_rows[16 + 4 * quad : 20 + 4 * quad, :].bitcast(I32),
             )
         key_planes = (ks_rows, ks_plane)
-
         nc.sync.dma_start(voffsets[:], voffs)
         for quad in range(4):
             nc.sync.dma_start(
                 vsc_pool[32 * quad : 32 * quad + 4, :].rearrange("r (u e) -> r u e", u=POOL_PAGES).bitcast(I32),
                 v_scales[:, 4 * quad : 4 * quad + 4, :].rearrange("u r e -> r u e").bitcast(I32),
             )
+        nc.sync.dma_start(vs_pool[:, SPREAD:], vs[:, SPREAD:])
         nc.sync.dma_start(
             vw_pool[:].rearrange("g (u e) -> g u e", u=POOL_PAGES),
             v_words.rearrange("u g e r -> g u (e r)").bitcast(I32),
         )
 
-        vs_view = vs_pool[:].rearrange("m (n c) -> m n c", c=T // P)
-        for blk in range(T // P // TILES):
+        vs_view = vs_pool[:, :SPREAD].rearrange("m (n c) -> m n c", c=SPREAD // P)
+        for blk in range(SPREAD // P // TILES):
             spread = ps.tile([P, TILES, P], F32, name="spread%d" % blk, tag="score%d" % (blk % PAGES))
             for j in range(TILES):
                 c = blk * TILES + j
@@ -133,11 +139,11 @@ def tile_attend_pkv4q_soft_cap_kb_kernel(
             nc.scalar.mul(half_kb[:, e * TILES : (e + 1) * TILES], kb_t[:, :, KB_ROW], 1.0 / CAP)
 
         sums = tile("sums", [P, HALVES], F32)
-        kw_g = [tile("kw_g%d" % e, [P, PAGE], U32) for e in range(PAGES)]
+        kw_g = [tile("kw_g%d" % e, [P, PAGE], U32)[:] for e in range(PAGES)]
         k4 = [tile("k4_%d" % h, [P, PASSES, 2 * HALF], U8) for h in range(HALVES)]
 
         def gather_keys(e):
-            nc.vector.tensor_copy(kw_g[e][:], kw_pool[:].bitcast(U32).indirect(page_offsets(e)))
+            nc.vector.tensor_copy(kw_g[e], kw_pool[:].bitcast(U32).indirect(page_offsets(e)))
 
         def part_keys(h):
             words = kw_g[h // 2][:, h % 2 * HALF : (h % 2 + 1) * HALF]
@@ -177,9 +183,8 @@ def tile_attend_pkv4q_soft_cap_kb_kernel(
 
         vsc_g = tile("vsc_g", [P, PAGES * DV], U8, tag="kw_g%d" % (PAGES - 1))
         nc.vector.tensor_copy(vsc_g[:], vsc_pool[:].indirect(voffsets[:]))
-        products = tile("products", [P, N + HALVES], F32, tag="vsc_pool")
-        tops = products[:, N : N + HALVES - 1]
-        total = products[:, N + HALVES - 1 :]
+        products = tile("products", [P, N + HALVES - 1], F32, tag="vsc_pool")
+        tops = products[:, N:]
         top = tile("top", [P, 1], F32)
         inv_top = tile("inv_top", [P, 1], F32)
         scaled = [products[:, e * PAGE : (e + 1) * PAGE] for e in range(PAGES)]
@@ -188,12 +193,14 @@ def tile_attend_pkv4q_soft_cap_kb_kernel(
                 nc.vector.tensor_reduce(tops[:, h : h + 1], expc[h][:], AX.X, ALU.max)
             else:
                 nc.vector.tensor_reduce(top[:], expc[h][:], AX.X, ALU.max)
-                nc.vector.reciprocal(inv_top[:], top[:])
             w0 = scaled[h // 2][:, h % 2 * HALF : (h % 2 + 1) * HALF]
             nc.vector.tensor_tensor(w0, vs_pool[:].indirect(half_offsets(h)), expc[h][:, :HALF], ALU.mult)
+            if h == HALVES - 1:
+                nc.vector.reciprocal(inv_top[:], top[:])
             if h == HALVES - 2:
                 nc.vector.tensor_reduce(expc[-1][:, HALF : HALF + 1], tops, AX.X, ALU.max)
 
+        total = tile("total", [P, 1], F32, tag="ex%d" % (HALVES - 2))
         ratio = tile("ratio", [P, 1], F32)
         factor = tile("factor", [P, 1], F32)
 
@@ -206,10 +213,6 @@ def tile_attend_pkv4q_soft_cap_kb_kernel(
             else:
                 nc.vector.tensor_scalar_mul(wb[:], source, inv_top[:])
             rounded.append(wb)
-
-        nc.vector.tensor_reduce(total, sums[:], AX.X, ALU.add)
-        nc.vector.tensor_tensor(ratio[:], total, inv_top[:], ALU.mult)
-        nc.vector.reciprocal(factor[:], ratio[:])
 
         vw_g = tile("vw_g", [P, PAGES * DV], U32, tag="vsc_pool")
         nc.vector.tensor_copy(vw_g[:], vw_pool[:].bitcast(U32).indirect(voffsets[:]))
@@ -236,6 +239,10 @@ def tile_attend_pkv4q_soft_cap_kb_kernel(
                 start=(e == 0),
                 stop=(e == PAGES - 1),
             )
+            if e == 0:
+                nc.vector.tensor_reduce(total[:], sums[:], AX.X, ALU.add)
+                nc.vector.tensor_tensor(ratio[:], total[:], inv_top[:], ALU.mult)
+                nc.vector.reciprocal(factor[:], ratio[:])
 
         result = tile("result", [P, DV], F32)
         nc.scalar.activation(result[:], acc[:], ACT.Copy, scale=factor[:])

@@ -15,8 +15,8 @@ KB_ROW = P - 1
 HALF = PAGE // 2
 HALVES = N // HALF
 SCORE_BANKS = 3
-KW_CUTS = (0, T // 2, T)
-SPREAD = T // 2
+KW_CUTS = (0, T // 8, T // 2, T)
+SPREAD = T
 
 FLOPS = 2 * NQ * N * (D + DV)
 
@@ -91,16 +91,19 @@ def tile_attend_pkv4q_soft_cap_kb_kernel(
 
         vs_rows = tile("vs_rows", [P, SPREAD // P], F32)
         nc.sync.dma_start(offsets[:], offs)
-        nc.sync.dma_start(vs_rows[:], vs[0, :SPREAD].rearrange("(p c) -> p c", p=P))
+        load_key_words(0)
         nc.sync.dma_start(ks_pool[0:32, :].bitcast(I32), ks_flat)
         for quad in (1, 2, 3):
             nc.sync.dma_start(ks_pool[32 * quad : 32 * quad + 4, :].bitcast(I32), ks_flat[4 * quad : 4 * quad + 4, :])
+        nc.sync.dma_start(vs_rows[:], vs[0, :SPREAD].rearrange("(p c) -> p c", p=P))
         nc.sync.dma_start(kb_pool[KB_ROW : KB_ROW + 1, :], kb[0:1, :])
-        load_key_words(0)
-        nc.sync.dma_start(qw[:], q_words[0].rearrange("o g q r -> g o (q r)").bitcast(I32))
-        for quad in range(4):
-            load_q_scales(quad)
         load_key_words(1)
+        load_q_scales(0)
+        load_q_scales(1)
+        load_key_words(2)
+        nc.sync.dma_start(qw[:], q_words[0].rearrange("o g q r -> g o (q r)").bitcast(I32))
+        load_q_scales(2)
+        load_q_scales(3)
 
         nc.vector.tensor_copy(ks_rows[:], ks_pool[:].indirect(offsets[:]))
         for quad in range(4):
@@ -115,7 +118,6 @@ def tile_attend_pkv4q_soft_cap_kb_kernel(
                 vsc_pool[32 * quad : 32 * quad + 4, :].rearrange("r (u e) -> r u e", u=POOL_PAGES).bitcast(I32),
                 v_scales[:, 4 * quad : 4 * quad + 4, :].rearrange("u r e -> r u e").bitcast(I32),
             )
-        nc.sync.dma_start(vs_pool[:, SPREAD:], vs[:, SPREAD:])
         nc.sync.dma_start(
             vw_pool[:].rearrange("g (u e) -> g u e", u=POOL_PAGES),
             v_words.rearrange("u g e r -> g u (e r)").bitcast(I32),
@@ -193,10 +195,9 @@ def tile_attend_pkv4q_soft_cap_kb_kernel(
                 nc.vector.tensor_reduce(tops[:, h : h + 1], expc[h][:], AX.X, ALU.max)
             else:
                 nc.vector.tensor_reduce(top[:], expc[h][:], AX.X, ALU.max)
+                nc.vector.reciprocal(inv_top[:], top[:])
             w0 = scaled[h // 2][:, h % 2 * HALF : (h % 2 + 1) * HALF]
             nc.vector.tensor_tensor(w0, vs_pool[:].indirect(half_offsets(h)), expc[h][:, :HALF], ALU.mult)
-            if h == HALVES - 1:
-                nc.vector.reciprocal(inv_top[:], top[:])
             if h == HALVES - 2:
                 nc.vector.tensor_reduce(expc[-1][:, HALF : HALF + 1], tops, AX.X, ALU.max)
 

@@ -15,7 +15,9 @@ KB_ROW = P - 1
 HALF = PAGE // 2
 HALVES = N // HALF
 SCORE_BANKS = 3
-KW_CUTS = (0, T // 8, T // 2, T)
+KW_CUTS = (0, 5 * T // 16, T)
+KB_SPLIT = 1344
+KS_ROW = 96
 SPREAD = T
 
 FLOPS = 2 * NQ * N * (D + DV)
@@ -51,23 +53,22 @@ def tile_attend_pkv4q_soft_cap_kb_kernel(
         kb_pool = tile("kb_pool", [P, T], F32)
         vs_pool = tile("vs_pool", [P, T], F32)
         vw_pool = tile("vw_pool", [P, POOL_PAGES * DV], I32)
-        vsc_pool = tile("vsc_pool", [P, POOL_PAGES * DV], U8)
         qw = tile("qw", [P, PASSES, NQ], I32)
         qs = tile("qs", [P, PASSES, NQ], U8)
         ks_rows = tile("ks_rows", [P, N], U8)
-        ks_plane = tile("ks_plane", [P, N], U8)
+        ks_plane = tile("ks_plane", [P, PASSES, N], U8)
         ident = tile("ident", [P, P], F32)
 
-        expc = [tile("ex%d" % h, [P, HALF + (2 if h == HALVES - 1 else 0)], F32) for h in range(HALVES)]
-        floor = expc[-1][:, HALF + 1 :]
-
-        def half_offsets(h):
-            return offsets[:, h * HALF // 16 : (h + 1) * HALF // 16]
+        vsc_pool = tile("vsc_pool", [P, POOL_PAGES * DV], U8)
+        vsc_rows = tile("vsc_rows", [P, PAGES * DV], U8)
+        vsc_plane = tile("vsc_plane", [P, PAGES * DV], U8)
+        early = [tile("ex%d" % e, [P, PAGE + 1 - e], F32) for e in range(PAGES - 1)]
+        fifth = tile("fifth", [P, HALF], F32)
+        floor = early[0][:, PAGE:]
 
         def page_offsets(e):
             return offsets[:, e * PAGE // 16 : (e + 1) * PAGE // 16]
 
-        ks_flat = k_scales.rearrange("o f t -> (o f) t").bitcast(I32)
         kw_flat = k_words[0].rearrange("g t b -> g (t b)").bitcast(I32)
 
         def load_q_scales(quad):
@@ -76,13 +77,13 @@ def tile_attend_pkv4q_soft_cap_kb_kernel(
                 q_scales[0, :, 4 * quad : 4 * quad + 4, :].rearrange("o r q -> r o q").bitcast(I32),
             )
 
-        nc.vector.memset(ks_pool[:].bitcast(I32), 0)
-        nc.vector.memset(floor, -CAP)
-        nc.vector.memset(qs[:].bitcast(I32), 0)
-        nc.vector.memset(kb_pool[:KB_ROW, :].bitcast(I32), 0)
-        nc.vector.memset(ks_plane[:].bitcast(I32), 0)
+        nc.vector.memset(ident[:], 0.0)
         nc.vector.memset(vsc_pool[:].bitcast(I32), 0)
-        make_identity(nc, ident[:])
+        nc.vector.memset(floor, -CAP)
+        nc.vector.memset(ks_pool[:KS_ROW, :].bitcast(I32), 0)
+        nc.vector.memset(kb_pool[:KB_ROW, :KB_SPLIT].bitcast(I32), 0)
+        make_identity(nc, ident[:], nomemset=True)
+        nc.gpsimd.memset(kb_pool[:KB_ROW, KB_SPLIT - 8 :].bitcast(I32), 0)
         nc.scalar.activation(floor, floor, ACT.Exp)
 
         def load_key_words(piece):
@@ -90,33 +91,34 @@ def tile_attend_pkv4q_soft_cap_kb_kernel(
             nc.sync.dma_start(kw_pool[:, cols], kw_flat[:, cols])
 
         vs_rows = tile("vs_rows", [P, SPREAD // P], F32)
+        nc.sync.dma_start(ks_pool[KS_ROW:, :].bitcast(I32), k_scales.rearrange("o f t -> f o t").bitcast(I32))
         nc.sync.dma_start(offsets[:], offs)
-        load_key_words(0)
-        nc.sync.dma_start(ks_pool[0:32, :].bitcast(I32), ks_flat)
-        for quad in (1, 2, 3):
-            nc.sync.dma_start(ks_pool[32 * quad : 32 * quad + 4, :].bitcast(I32), ks_flat[4 * quad : 4 * quad + 4, :])
         nc.sync.dma_start(vs_rows[:], vs[0, :SPREAD].rearrange("(p c) -> p c", p=P))
+        load_key_words(0)
+        nc.sync.dma_start(
+            vsc_pool[0:P:8, :].rearrange("f (u e) -> f u e", u=POOL_PAGES).bitcast(I32),
+            v_scales.rearrange("u f e -> f u e").bitcast(I32),
+        )
+        nc.sync.dma_start(voffsets[:], voffs)
         nc.sync.dma_start(kb_pool[KB_ROW : KB_ROW + 1, :], kb[0:1, :])
-        load_key_words(1)
         load_q_scales(0)
         load_q_scales(1)
-        load_key_words(2)
+        load_key_words(1)
         nc.sync.dma_start(qw[:], q_words[0].rearrange("o g q r -> g o (q r)").bitcast(I32))
         load_q_scales(2)
         load_q_scales(3)
 
         nc.vector.tensor_copy(ks_rows[:], ks_pool[:].indirect(offsets[:]))
+        nc.vector.tensor_copy(vsc_rows[:], vsc_pool[:].indirect(voffsets[:]))
         for quad in range(4):
             nc.sync.dma_start(
-                ks_plane[32 * quad : 32 * quad + 4, :].bitcast(I32),
-                ks_rows[16 + 4 * quad : 20 + 4 * quad, :].bitcast(I32),
+                ks_plane[32 * quad : 32 * quad + 4, :, :].bitcast(I32),
+                ks_rows[KS_ROW + 8 * quad : KS_ROW + 8 * quad + 8, :].bitcast(I32),
             )
-        key_planes = (ks_rows, ks_plane)
-        nc.sync.dma_start(voffsets[:], voffs)
         for quad in range(4):
             nc.sync.dma_start(
-                vsc_pool[32 * quad : 32 * quad + 4, :].rearrange("r (u e) -> r u e", u=POOL_PAGES).bitcast(I32),
-                v_scales[:, 4 * quad : 4 * quad + 4, :].rearrange("u r e -> r u e").bitcast(I32),
+                vsc_plane[32 * quad : 32 * quad + 4, :].bitcast(I32),
+                vsc_rows[32 * quad : 32 * quad + 32 : 8, :].bitcast(I32),
             )
         nc.sync.dma_start(
             vw_pool[:].rearrange("g (u e) -> g u e", u=POOL_PAGES),
@@ -157,6 +159,11 @@ def tile_attend_pkv4q_soft_cap_kb_kernel(
             if h % 2 == 0 and h // 2 + 1 < PAGES:
                 gather_keys(h // 2 + 1)
 
+        products = tile("products", [P, N + HALF + 4], F32, tag="kw_g%d" % (PAGES - 1))
+        last = products[:, N:]
+        expc = [early[h // 2][:, h % 2 * HALF : (h % 2 + 1) * HALF] for h in range(HALVES - 2)]
+        expc.extend([fifth[:], last[:, :HALF]])
+
         for h in range(HALVES):
             s_t = ps.tile([P, 2, NQ], F32, name="s_t%d" % h, tag="score%d" % (h % SCORE_BANKS))
             for j in range(2):
@@ -164,7 +171,7 @@ def tile_attend_pkv4q_soft_cap_kb_kernel(
                     nc.tensor.matmul_mx(
                         out=s_t[:, j, :],
                         lhsT=k4[h][:, o, 2 * j * P : 2 * (j + 1) * P].bitcast(FP4X4),
-                        lhsT_scale=key_planes[o][:, h * HALF + j * P : h * HALF + (j + 1) * P],
+                        lhsT_scale=ks_plane[:, o, h * HALF + j * P : h * HALF + (j + 1) * P],
                         rhs=qw[:, o, :].bitcast(FP8X4),
                         rhs_scale=qs[:, o, :],
                         start=(o == 0),
@@ -180,50 +187,46 @@ def tile_attend_pkv4q_soft_cap_kb_kernel(
             for j in range(2):
                 nc.tensor.transpose(th[:, j, :], th_t[:, j, :], ident[:])
             nc.scalar.activation(
-                expc[h][:, :HALF], th[:].rearrange("q j k -> q (j k)"), ACT.Exp, scale=CAP, accum_out=sums[:, h : h + 1]
+                expc[h], th[:].rearrange("q j k -> q (j k)"), ACT.Exp, scale=CAP, accum_out=sums[:, h : h + 1]
             )
 
-        vsc_g = tile("vsc_g", [P, PAGES * DV], U8, tag="kw_g%d" % (PAGES - 1))
-        nc.vector.tensor_copy(vsc_g[:], vsc_pool[:].indirect(voffsets[:]))
-        products = tile("products", [P, N + HALVES - 1], F32, tag="vsc_pool")
-        tops = products[:, N:]
-        top = tile("top", [P, 1], F32)
-        inv_top = tile("inv_top", [P, 1], F32)
-        scaled = [products[:, e * PAGE : (e + 1) * PAGE] for e in range(PAGES)]
-        for h in range(HALVES):
-            if h < HALVES - 1:
-                nc.vector.tensor_reduce(tops[:, h : h + 1], expc[h][:], AX.X, ALU.max)
-            else:
-                nc.vector.tensor_reduce(top[:], expc[h][:], AX.X, ALU.max)
-                nc.vector.reciprocal(inv_top[:], top[:])
-            w0 = scaled[h // 2][:, h % 2 * HALF : (h % 2 + 1) * HALF]
-            nc.vector.tensor_tensor(w0, vs_pool[:].indirect(half_offsets(h)), expc[h][:, :HALF], ALU.mult)
-            if h == HALVES - 2:
-                nc.vector.tensor_reduce(expc[-1][:, HALF : HALF + 1], tops, AX.X, ALU.max)
-
-        total = tile("total", [P, 1], F32, tag="ex%d" % (HALVES - 2))
-        ratio = tile("ratio", [P, 1], F32)
+        stats = tile("stats", [P, 2], F32)
+        inv = tile("inv", [P, 2], F32)
+        top, total = stats[:, 0:1], stats[:, 1:2]
+        inv_top, inv_total = inv[:, 0:1], inv[:, 1:2]
+        sums_copy = tile("sums_copy", [P, HALVES], F32)
         factor = tile("factor", [P, 1], F32)
+        chunks = [(0, PAGE, early[0][:]), (PAGE, PAGE, early[1][:]), (2 * PAGE, HALF, fifth[:])]
+        for i, (c0, n, ex) in enumerate(chunks):
+            nc.vector.tensor_reduce(last[:, HALF + i : HALF + i + 1], ex, AX.X, ALU.max)
+            nc.vector.tensor_tensor(
+                products[:, c0 : c0 + n], vs_pool[:].indirect(offsets[:, c0 // 16 : (c0 + n) // 16]), ex[:, :n], ALU.mult
+            )
+        nc.scalar.activation(sums_copy[:], sums[:], ACT.Copy, accum_out=total)
+        nc.vector.tensor_reduce(top, last[:, : HALF + len(chunks)], AX.X, ALU.max)
+        nc.vector.reciprocal(inv[:], stats[:])
+        nc.vector.tensor_tensor(
+            products[:, N - HALF : N], vs_pool[:].indirect(offsets[:, (N - HALF) // 16 :]), last[:, :HALF], ALU.mult
+        )
 
-        rounded = []
-        for e in range(PAGES):
-            wb = tile("wb%d" % e, [P, 2, P, 2], BF16)
-            source = scaled[e].rearrange("q (g u c) -> q u g c", u=2, c=2)
-            if e == 0:
-                nc.scalar.activation(wb[:], source, ACT.Copy, scale=inv_top[:])
-            else:
-                nc.vector.tensor_scalar_mul(wb[:], source, inv_top[:])
-            rounded.append(wb)
+        wb0 = tile("wb0", [P, 2, P, 2], BF16)
+        wb12 = tile("wb12", [P, 2, 2 * P, 2], BF16)
+        nc.scalar.activation(
+            wb0[:], products[:, :PAGE].rearrange("q (g u c) -> q u g c", u=2, c=2), ACT.Copy, scale=inv_top
+        )
+        nc.vector.tensor_scalar_mul(wb12[:], products[:, PAGE:N].rearrange("q (g u c) -> q u g c", u=2, c=2), inv_top)
+        words0 = wb0[:].rearrange("q u g c -> q u (g c)").bitcast(F32)
+        words12 = wb12[:].rearrange("q u g c -> q u (g c)").bitcast(F32)
+        words = [words0, words12[:, :, :P], words12[:, :, P:]]
 
-        vw_g = tile("vw_g", [P, PAGES * DV], U32, tag="vsc_pool")
+        vw_g = tile("vw_g", [P, PAGES * DV], U32, tag="kw_g%d" % (PAGES - 1))
         nc.vector.tensor_copy(vw_g[:], vw_pool[:].bitcast(U32).indirect(voffsets[:]))
 
         acc = ps.tile([P, DV], F32, name="acc", tag="acc")
         for e in range(PAGES):
-            words = rounded[e][:].rearrange("q u g c -> q (u g c)").bitcast(F32)
             w_t = ps.tile([P, 2, NQ], F32, name="w_t%d" % e, tag="score%d" % e)
             for u in range(2):
-                nc.tensor.transpose(w_t[:, u, :], words[:, u * P : (u + 1) * P], ident[:])
+                nc.tensor.transpose(w_t[:, u, :], words[e][:, u, :], ident[:])
             wq = tile("wq%d" % e, [P, 4 * NQ], BF16)
             nc.scalar.copy(
                 wq[:].bitcast(F32).rearrange("g (q u) -> g q u", u=2), w_t[:].rearrange("g u q -> g q u")
@@ -236,15 +239,12 @@ def tile_attend_pkv4q_soft_cap_kb_kernel(
                 lhsT=codes[:].bitcast(FP8X4),
                 lhsT_scale=scales[:],
                 rhs=vw_g[:, e * DV : (e + 1) * DV].bitcast(FP8X4),
-                rhs_scale=vsc_g[:, e * DV : (e + 1) * DV],
+                rhs_scale=vsc_plane[:, e * DV : (e + 1) * DV],
                 start=(e == 0),
                 stop=(e == PAGES - 1),
             )
-            if e == 0:
-                nc.vector.tensor_reduce(total[:], sums[:], AX.X, ALU.add)
-                nc.vector.tensor_tensor(ratio[:], total[:], inv_top[:], ALU.mult)
-                nc.vector.reciprocal(factor[:], ratio[:])
 
+        nc.scalar.activation(factor[:], inv_total, ACT.Copy, scale=top)
         result = tile("result", [P, DV], F32)
         nc.scalar.activation(result[:], acc[:], ACT.Copy, scale=factor[:])
         nc.sync.dma_start(out[0], result[:])

@@ -15,10 +15,10 @@ KB_ROW = P - 1
 HALF = PAGE // 2
 HALVES = N // HALF
 SCORE_BANKS = 3
-KW_CUTS = (0, 5 * T // 16, T)
-KB_SPLIT = 1344
+KW_CUTS = (0, 3 * T // 16, T // 2, T)
+KB_SPLIT = 1792
 KS_ROW = 96
-SPREAD = T
+SPREAD = 3 * T // 4
 
 FLOPS = 2 * NQ * N * (D + DV)
 
@@ -60,11 +60,11 @@ def tile_attend_pkv4q_soft_cap_kb_kernel(
         ident = tile("ident", [P, P], F32)
 
         vsc_pool = tile("vsc_pool", [P, POOL_PAGES * DV], U8)
-        vsc_rows = tile("vsc_rows", [P, PAGES * DV], U8)
+        vsc_first = tile("vsc_first", [P, DV], U8)
         vsc_plane = tile("vsc_plane", [P, PAGES * DV], U8)
-        early = [tile("ex%d" % e, [P, PAGE + 1 - e], F32) for e in range(PAGES - 1)]
-        fifth = tile("fifth", [P, HALF], F32)
-        floor = early[0][:, PAGE:]
+        first = tile("first", [P, HALF + 1], F32)
+        middle = [tile("middle%d" % i, [P, PAGE], F32) for i in range(PAGES - 1)]
+        floor = first[:, HALF:]
 
         def page_offsets(e):
             return offsets[:, e * PAGE // 16 : (e + 1) * PAGE // 16]
@@ -91,9 +91,9 @@ def tile_attend_pkv4q_soft_cap_kb_kernel(
             nc.sync.dma_start(kw_pool[:, cols], kw_flat[:, cols])
 
         vs_rows = tile("vs_rows", [P, SPREAD // P], F32)
+        nc.sync.dma_start(vs_rows[:], vs[0, :SPREAD].rearrange("(p c) -> p c", p=P))
         nc.sync.dma_start(ks_pool[KS_ROW:, :].bitcast(I32), k_scales.rearrange("o f t -> f o t").bitcast(I32))
         nc.sync.dma_start(offsets[:], offs)
-        nc.sync.dma_start(vs_rows[:], vs[0, :SPREAD].rearrange("(p c) -> p c", p=P))
         load_key_words(0)
         nc.sync.dma_start(
             vsc_pool[0:P:8, :].rearrange("f (u e) -> f u e", u=POOL_PAGES).bitcast(I32),
@@ -101,25 +101,31 @@ def tile_attend_pkv4q_soft_cap_kb_kernel(
         )
         nc.sync.dma_start(voffsets[:], voffs)
         nc.sync.dma_start(kb_pool[KB_ROW : KB_ROW + 1, :], kb[0:1, :])
+        load_key_words(1)
         load_q_scales(0)
         load_q_scales(1)
-        load_key_words(1)
+        load_key_words(2)
         nc.sync.dma_start(qw[:], q_words[0].rearrange("o g q r -> g o (q r)").bitcast(I32))
         load_q_scales(2)
         load_q_scales(3)
 
         nc.vector.tensor_copy(ks_rows[:], ks_pool[:].indirect(offsets[:]))
-        nc.vector.tensor_copy(vsc_rows[:], vsc_pool[:].indirect(voffsets[:]))
-        for quad in range(4):
+        nc.vector.tensor_copy(vsc_first[:], vsc_pool[:].indirect(voffsets[:, : DV // 16]))
+        for quad in (0, 2, 1, 3):
             nc.sync.dma_start(
                 ks_plane[32 * quad : 32 * quad + 4, :, :].bitcast(I32),
                 ks_rows[KS_ROW + 8 * quad : KS_ROW + 8 * quad + 8, :].bitcast(I32),
             )
-        for quad in range(4):
-            nc.sync.dma_start(
-                vsc_plane[32 * quad : 32 * quad + 4, :].bitcast(I32),
-                vsc_rows[32 * quad : 32 * quad + 32 : 8, :].bitcast(I32),
-            )
+
+        def move_value_scales(rows, c0):
+            for quad in range(4):
+                nc.sync.dma_start(
+                    vsc_plane[32 * quad : 32 * quad + 4, c0 : c0 + rows.shape[1]].bitcast(I32),
+                    rows[32 * quad : 32 * quad + 32 : 8, :].bitcast(I32),
+                )
+
+        nc.sync.dma_start(vs_pool[:, SPREAD:], vs[:, SPREAD:])
+        move_value_scales(vsc_first, 0)
         nc.sync.dma_start(
             vw_pool[:].rearrange("g (u e) -> g u e", u=POOL_PAGES),
             v_words.rearrange("u g e r -> g u (e r)").bitcast(I32),
@@ -159,10 +165,14 @@ def tile_attend_pkv4q_soft_cap_kb_kernel(
             if h % 2 == 0 and h // 2 + 1 < PAGES:
                 gather_keys(h // 2 + 1)
 
-        products = tile("products", [P, N + HALF + 4], F32, tag="kw_g%d" % (PAGES - 1))
+        vsc_rest = tile("vsc_rest", [P, (PAGES - 1) * DV], U8, tag="kw_g%d" % (PAGES - 1))
+        nc.vector.tensor_copy(vsc_rest[:], vsc_pool[:].indirect(voffsets[:, DV // 16 :]))
+        move_value_scales(vsc_rest, DV)
+        products = tile("products", [P, N + HALF + 4], F32, tag="vsc_pool")
         last = products[:, N:]
-        expc = [early[h // 2][:, h % 2 * HALF : (h % 2 + 1) * HALF] for h in range(HALVES - 2)]
-        expc.extend([fifth[:], last[:, :HALF]])
+        expc = [first[:, :HALF]]
+        expc.extend([middle[h // 2][:, h % 2 * HALF : (h % 2 + 1) * HALF] for h in range(HALVES - 2)])
+        expc.append(last[:, :HALF])
 
         for h in range(HALVES):
             s_t = ps.tile([P, 2, NQ], F32, name="s_t%d" % h, tag="score%d" % (h % SCORE_BANKS))
@@ -196,7 +206,7 @@ def tile_attend_pkv4q_soft_cap_kb_kernel(
         inv_top, inv_total = inv[:, 0:1], inv[:, 1:2]
         sums_copy = tile("sums_copy", [P, HALVES], F32)
         factor = tile("factor", [P, 1], F32)
-        chunks = [(0, PAGE, early[0][:]), (PAGE, PAGE, early[1][:]), (2 * PAGE, HALF, fifth[:])]
+        chunks = [(0, HALF, first[:]), (HALF, PAGE, middle[0][:]), (HALF + PAGE, PAGE, middle[1][:])]
         for i, (c0, n, ex) in enumerate(chunks):
             nc.vector.tensor_reduce(last[:, HALF + i : HALF + i + 1], ex, AX.X, ALU.max)
             nc.vector.tensor_tensor(
@@ -204,22 +214,22 @@ def tile_attend_pkv4q_soft_cap_kb_kernel(
             )
         nc.scalar.activation(sums_copy[:], sums[:], ACT.Copy, accum_out=total)
         nc.vector.tensor_reduce(top, last[:, : HALF + len(chunks)], AX.X, ALU.max)
-        nc.vector.reciprocal(inv[:], stats[:])
         nc.vector.tensor_tensor(
             products[:, N - HALF : N], vs_pool[:].indirect(offsets[:, (N - HALF) // 16 :]), last[:, :HALF], ALU.mult
         )
+        nc.vector.reciprocal(inv[:], stats[:])
 
-        wb0 = tile("wb0", [P, 2, P, 2], BF16)
-        wb12 = tile("wb12", [P, 2, 2 * P, 2], BF16)
-        nc.scalar.activation(
-            wb0[:], products[:, :PAGE].rearrange("q (g u c) -> q u g c", u=2, c=2), ACT.Copy, scale=inv_top
-        )
-        nc.vector.tensor_scalar_mul(wb12[:], products[:, PAGE:N].rearrange("q (g u c) -> q u g c", u=2, c=2), inv_top)
-        words0 = wb0[:].rearrange("q u g c -> q u (g c)").bitcast(F32)
-        words12 = wb12[:].rearrange("q u g c -> q u (g c)").bitcast(F32)
-        words = [words0, words12[:, :, :P], words12[:, :, P:]]
+        words = []
+        for e in range(PAGES):
+            wb = tile("wb%d" % e, [P, 2, P, 2], BF16)
+            source = products[:, e * PAGE : (e + 1) * PAGE].rearrange("q (g u c) -> q u g c", u=2, c=2)
+            if e == 1:
+                nc.scalar.activation(wb[:], source, ACT.Copy, scale=inv_top)
+            else:
+                nc.vector.tensor_scalar_mul(wb[:], source, inv_top)
+            words.append(wb[:].rearrange("q u g c -> q u (g c)").bitcast(F32))
 
-        vw_g = tile("vw_g", [P, PAGES * DV], U32, tag="kw_g%d" % (PAGES - 1))
+        vw_g = tile("vw_g", [P, PAGES * DV], U32, tag="vsc_pool")
         nc.vector.tensor_copy(vw_g[:], vw_pool[:].bitcast(U32).indirect(voffsets[:]))
 
         acc = ps.tile([P, DV], F32, name="acc", tag="acc")

@@ -16,8 +16,8 @@ HALF = PAGE // 2
 HALVES = N // HALF
 SCORE_BANKS = 3
 KW_CUTS = (0, 3 * T // 16, T // 2, T)
-KB_SPLIT = 1792
 KS_ROW = 96
+KB_FIRST = 256
 SPREAD = 3 * T // 4
 
 FLOPS = 2 * NQ * N * (D + DV)
@@ -60,7 +60,7 @@ def tile_attend_pkv4q_soft_cap_kb_kernel(
         ident = tile("ident", [P, P], F32)
 
         vsc_pool = tile("vsc_pool", [P, POOL_PAGES * DV], U8)
-        vsc_first = tile("vsc_first", [P, DV], U8)
+        vsc_rows = tile("vsc_rows", [P, PAGES * DV], U8)
         vsc_plane = tile("vsc_plane", [P, PAGES * DV], U8)
         first = tile("first", [P, HALF + 1], F32)
         middle = [tile("middle%d" % i, [P, PAGE], F32) for i in range(PAGES - 1)]
@@ -77,13 +77,17 @@ def tile_attend_pkv4q_soft_cap_kb_kernel(
                 q_scales[0, :, 4 * quad : 4 * quad + 4, :].rearrange("o r q -> r o q").bitcast(I32),
             )
 
-        nc.vector.memset(ident[:], 0.0)
-        nc.vector.memset(vsc_pool[:].bitcast(I32), 0)
+        def zero_words(words):
+            half = words.shape[1] // 2 + 1
+            nc.vector.memset(words[:, :half], 0)
+            nc.vector.memset(words[:, half:], 0)
+
+        make_identity(nc, ident[:])
+        nc.gpsimd.memset(kb_pool[:KB_ROW, :KB_FIRST].bitcast(I32), 0)
+        nc.gpsimd.memset(kb_pool[:KB_ROW, KB_FIRST:].bitcast(I32), 0)
         nc.vector.memset(floor, -CAP)
-        nc.vector.memset(ks_pool[:KS_ROW, :].bitcast(I32), 0)
-        nc.vector.memset(kb_pool[:KB_ROW, :KB_SPLIT].bitcast(I32), 0)
-        make_identity(nc, ident[:], nomemset=True)
-        nc.gpsimd.memset(kb_pool[:KB_ROW, KB_SPLIT - 8 :].bitcast(I32), 0)
+        zero_words(vsc_pool[:].bitcast(I32))
+        zero_words(ks_pool[:KS_ROW, :].bitcast(I32))
         nc.scalar.activation(floor, floor, ACT.Exp)
 
         def load_key_words(piece):
@@ -91,9 +95,9 @@ def tile_attend_pkv4q_soft_cap_kb_kernel(
             nc.sync.dma_start(kw_pool[:, cols], kw_flat[:, cols])
 
         vs_rows = tile("vs_rows", [P, SPREAD // P], F32)
-        nc.sync.dma_start(vs_rows[:], vs[0, :SPREAD].rearrange("(p c) -> p c", p=P))
-        nc.sync.dma_start(ks_pool[KS_ROW:, :].bitcast(I32), k_scales.rearrange("o f t -> f o t").bitcast(I32))
+        nc.scalar.dma_start(ks_pool[KS_ROW:, :].bitcast(I32), k_scales.rearrange("o f t -> f o t").bitcast(I32))
         nc.sync.dma_start(offsets[:], offs)
+        nc.sync.dma_start(vs_rows[:], vs[0, :SPREAD].rearrange("(p c) -> p c", p=P))
         load_key_words(0)
         nc.sync.dma_start(
             vsc_pool[0:P:8, :].rearrange("f (u e) -> f u e", u=POOL_PAGES).bitcast(I32),
@@ -110,22 +114,18 @@ def tile_attend_pkv4q_soft_cap_kb_kernel(
         load_q_scales(3)
 
         nc.vector.tensor_copy(ks_rows[:], ks_pool[:].indirect(offsets[:]))
-        nc.vector.tensor_copy(vsc_first[:], vsc_pool[:].indirect(voffsets[:, : DV // 16]))
+        nc.vector.tensor_copy(vsc_rows[:], vsc_pool[:].indirect(voffsets[:]))
         for quad in (0, 2, 1, 3):
             nc.sync.dma_start(
                 ks_plane[32 * quad : 32 * quad + 4, :, :].bitcast(I32),
                 ks_rows[KS_ROW + 8 * quad : KS_ROW + 8 * quad + 8, :].bitcast(I32),
             )
-
-        def move_value_scales(rows, c0):
-            for quad in range(4):
-                nc.sync.dma_start(
-                    vsc_plane[32 * quad : 32 * quad + 4, c0 : c0 + rows.shape[1]].bitcast(I32),
-                    rows[32 * quad : 32 * quad + 32 : 8, :].bitcast(I32),
-                )
-
         nc.sync.dma_start(vs_pool[:, SPREAD:], vs[:, SPREAD:])
-        move_value_scales(vsc_first, 0)
+        for quad in range(4):
+            nc.sync.dma_start(
+                vsc_plane[32 * quad : 32 * quad + 4, :].bitcast(I32),
+                vsc_rows[32 * quad : 32 * quad + 32 : 8, :].bitcast(I32),
+            )
         nc.sync.dma_start(
             vw_pool[:].rearrange("g (u e) -> g u e", u=POOL_PAGES),
             v_words.rearrange("u g e r -> g u (e r)").bitcast(I32),
@@ -140,9 +140,11 @@ def tile_attend_pkv4q_soft_cap_kb_kernel(
             nc.scalar.copy(vs_view[:, :, blk * TILES : (blk + 1) * TILES], spread[:].rearrange("m j n -> m n j"))
 
         half_kb = tile("half_kb", [P, PAGES * TILES], F32)
+        kb_all = tile("kb_all", [P, N], F32)
+        nc.vector.tensor_copy(kb_all[:, :PAGE], kb_pool[:].indirect(offsets[:, : PAGE // 16]))
+        nc.vector.tensor_copy(kb_all[:, PAGE:], kb_pool[:].indirect(offsets[:, PAGE // 16 :]))
         for e in range(PAGES):
-            kb_g = tile("kb_g%d" % e, [P, PAGE], F32)
-            nc.vector.tensor_copy(kb_g[:], kb_pool[:].indirect(page_offsets(e)))
+            kb_g = kb_all[:, e * PAGE : (e + 1) * PAGE]
             kb_t = ps.tile([P, TILES, P], F32, name="kb_t%d" % e, tag="turn%d" % e)
             for j in range(TILES):
                 nc.tensor.transpose(kb_t[:, j, :], kb_g[:, j * P : (j + 1) * P], ident[:])
@@ -165,10 +167,7 @@ def tile_attend_pkv4q_soft_cap_kb_kernel(
             if h % 2 == 0 and h // 2 + 1 < PAGES:
                 gather_keys(h // 2 + 1)
 
-        vsc_rest = tile("vsc_rest", [P, (PAGES - 1) * DV], U8, tag="kw_g%d" % (PAGES - 1))
-        nc.vector.tensor_copy(vsc_rest[:], vsc_pool[:].indirect(voffsets[:, DV // 16 :]))
-        move_value_scales(vsc_rest, DV)
-        products = tile("products", [P, N + HALF + 4], F32, tag="vsc_pool")
+        products = tile("products", [P, N + HALF + 4], F32, tag="kw_g%d" % (PAGES - 1))
         last = products[:, N:]
         expc = [first[:, :HALF]]
         expc.extend([middle[h // 2][:, h % 2 * HALF : (h % 2 + 1) * HALF] for h in range(HALVES - 2)])
@@ -229,7 +228,7 @@ def tile_attend_pkv4q_soft_cap_kb_kernel(
                 nc.vector.tensor_scalar_mul(wb[:], source, inv_top)
             words.append(wb[:].rearrange("q u g c -> q u (g c)").bitcast(F32))
 
-        vw_g = tile("vw_g", [P, PAGES * DV], U32, tag="vsc_pool")
+        vw_g = tile("vw_g", [P, PAGES * DV], U32, tag="kw_g%d" % (PAGES - 1))
         nc.vector.tensor_copy(vw_g[:], vw_pool[:].bitcast(U32).indirect(voffsets[:]))
 
         acc = ps.tile([P, DV], F32, name="acc", tag="acc")

@@ -18,7 +18,7 @@ SCORE_BANKS = 3
 KW_CUTS = (0, 3 * T // 16, T // 2, T)
 KS_ROW = 96
 KB_FIRST = 256
-SPREAD = 3 * T // 4
+SPREAD = T
 
 FLOPS = 2 * NQ * N * (D + DV)
 
@@ -120,7 +120,6 @@ def tile_attend_pkv4q_soft_cap_kb_kernel(
                 ks_plane[32 * quad : 32 * quad + 4, :, :].bitcast(I32),
                 ks_rows[KS_ROW + 8 * quad : KS_ROW + 8 * quad + 8, :].bitcast(I32),
             )
-        nc.sync.dma_start(vs_pool[:, SPREAD:], vs[:, SPREAD:])
         for quad in range(4):
             nc.sync.dma_start(
                 vsc_plane[32 * quad : 32 * quad + 4, :].bitcast(I32),
@@ -162,10 +161,12 @@ def tile_attend_pkv4q_soft_cap_kb_kernel(
             nc.vector.tensor_copy(k4[h][:].bitcast(U16), words.bitcast(U16).rearrange("g (n o) -> g o n", o=PASSES))
 
         gather_keys(0)
-        for h in range(HALVES):
+        gather_keys(1)
+        for h in range(HALVES - 2):
             part_keys(h)
-            if h % 2 == 0 and h // 2 + 1 < PAGES:
-                gather_keys(h // 2 + 1)
+        gather_keys(2)
+        part_keys(HALVES - 2)
+        part_keys(HALVES - 1)
 
         products = tile("products", [P, N + HALF + 4], F32, tag="kw_g%d" % (PAGES - 1))
         last = products[:, N:]

@@ -17,6 +17,7 @@ HALVES = N // HALF
 SCORE_BANKS = 3
 KW_CUTS = (0, 3 * T // 16, T // 2, T)
 KS_ROW = 96
+WARM_WIDTHS = (256, 256, 256, 128)
 KB_FIRST = 256
 SPREAD = T
 
@@ -173,6 +174,18 @@ def tile_attend_pkv4q_soft_cap_kb_kernel(
         expc = [first[:, :HALF]]
         expc.extend([middle[h // 2][:, h % 2 * HALF : (h % 2 + 1) * HALF] for h in range(HALVES - 2)])
         expc.append(last[:, :HALF])
+
+        warm = ps.tile([P, PASSES * NQ], F32, name="warm", tag="acc")
+        for width in WARM_WIDTHS:
+            nc.tensor.matmul_mx(
+                out=warm[:, :width],
+                lhsT=qw[:, 0, :].bitcast(FP8X4),
+                lhsT_scale=qs[:, 0, :],
+                rhs=qw[:].rearrange("g o q -> g (o q)")[:, :width].bitcast(FP8X4),
+                rhs_scale=qs[:].rearrange("g o q -> g (o q)")[:, :width],
+                start=True,
+                stop=True,
+            )
 
         for h in range(HALVES):
             s_t = ps.tile([P, 2, NQ], F32, name="s_t%d" % h, tag="score%d" % (h % SCORE_BANKS))

@@ -150,7 +150,6 @@ def tile_attend_pkv4q_soft_cap_kb_kernel(
                 nc.tensor.transpose(kb_t[:, j, :], kb_g[:, j * P : (j + 1) * P], ident[:])
             nc.scalar.mul(half_kb[:, e * TILES : (e + 1) * TILES], kb_t[:, :, KB_ROW], 1.0 / CAP)
 
-        sums = tile("sums", [P, HALVES], F32)
         kw_g = [tile("kw_g%d" % e, [P, PAGE], U32)[:] for e in range(PAGES)]
         k4 = [tile("k4_%d" % h, [P, PASSES, 2 * HALF], U8) for h in range(HALVES)]
 
@@ -209,28 +208,35 @@ def tile_attend_pkv4q_soft_cap_kb_kernel(
             th = ps.tile([P, 2, P], F32, name="th%d" % h, tag="turn%d" % (h % PAGES))
             for j in range(2):
                 nc.tensor.transpose(th[:, j, :], th_t[:, j, :], ident[:])
-            nc.scalar.activation(
-                expc[h], th[:].rearrange("q j k -> q (j k)"), ACT.Exp, scale=CAP, accum_out=sums[:, h : h + 1]
-            )
+            nc.scalar.activation(expc[h], th[:].rearrange("q j k -> q (j k)"), ACT.Exp, scale=CAP)
 
-        stats = tile("stats", [P, 2], F32)
-        inv = tile("inv", [P, 2], F32)
-        top, total = stats[:, 0:1], stats[:, 1:2]
-        inv_top, inv_total = inv[:, 0:1], inv[:, 1:2]
-        sums_copy = tile("sums_copy", [P, HALVES], F32)
-        factor = tile("factor", [P, 1], F32)
+        top = tile("top", [P, 1], F32)[:]
+        total = tile("total", [P, 1], F32)[:]
+        inv = tile("inv", [P, 1], F32)
+        inv_top = inv[:, 0:1]
+        folded = ps.tile([P, NQ], F32, name="folded", tag="turn%d" % ((HALVES - 1) % PAGES))
+        for t in range(N // P):
+            nc.tensor.matmul(
+                folded[:],
+                expc[t // 2][:, t % 2 * P : (t % 2 + 1) * P],
+                ident[:],
+                start=(t == 0),
+                stop=(t == N // P - 1),
+                is_transpose=True,
+            )
+        folded_sb = tile("folded_sb", [P, NQ], F32)
+        nc.scalar.copy(folded_sb[:], folded[:])
         chunks = [(0, HALF, first[:]), (HALF, PAGE, middle[0][:]), (HALF + PAGE, PAGE, middle[1][:])]
         for i, (c0, n, ex) in enumerate(chunks):
             nc.vector.tensor_reduce(last[:, HALF + i : HALF + i + 1], ex, AX.X, ALU.max)
             nc.vector.tensor_tensor(
                 products[:, c0 : c0 + n], vs_pool[:].indirect(offsets[:, c0 // 16 : (c0 + n) // 16]), ex[:, :n], ALU.mult
             )
-        nc.scalar.activation(sums_copy[:], sums[:], ACT.Copy, accum_out=total)
         nc.vector.tensor_reduce(top, last[:, : HALF + len(chunks)], AX.X, ALU.max)
         nc.vector.tensor_tensor(
             products[:, N - HALF : N], vs_pool[:].indirect(offsets[:, (N - HALF) // 16 :]), last[:, :HALF], ALU.mult
         )
-        nc.vector.reciprocal(inv[:], stats[:])
+        nc.vector.reciprocal(inv_top, top)
 
         words = []
         for e in range(PAGES):
@@ -267,7 +273,12 @@ def tile_attend_pkv4q_soft_cap_kb_kernel(
                 stop=(e == PAGES - 1),
             )
 
-        nc.scalar.activation(factor[:], inv_total, ACT.Copy, scale=top)
+        unfolded = ps.tile([P, P], F32, name="unfolded", tag="score0")
+        nc.tensor.transpose(unfolded[:], folded_sb[:], ident[:])
+        sums_copy = tile("sums_copy", [P, P], F32)
+        nc.scalar.activation(sums_copy[:], unfolded[:], ACT.Copy, accum_out=total)
+        inv_total = tile("inv_total", [P, 1], F32)[:]
+        nc.vector.reciprocal(inv_total, total)
         result = tile("result", [P, DV], F32)
-        nc.scalar.activation(result[:], acc[:], ACT.Copy, scale=factor[:])
+        nc.vector.tensor_scalar(result[:], acc[:], inv_total, top, ALU.mult, ALU.mult)
         nc.sync.dma_start(out[0], result[:])

@@ -151,14 +151,16 @@ def tile_attend_pkv4q_soft_cap_kb_kernel(
             nc.scalar.mul(half_kb[:, e * TILES : (e + 1) * TILES], kb_t[:, :, KB_ROW], 1.0 / CAP)
 
         kw_g = [tile("kw_g%d" % e, [P, PAGE], U32)[:] for e in range(PAGES)]
-        k4 = [tile("k4_%d" % h, [P, PASSES, 2 * HALF], U8) for h in range(HALVES)]
+        k4 = [tile("k4_%d" % h, [P, HALF // P, PASSES, 2 * P], U8) for h in range(HALVES)]
 
         def gather_keys(e):
             nc.vector.tensor_copy(kw_g[e], kw_pool[:].bitcast(U32).indirect(page_offsets(e)))
 
         def part_keys(h):
             words = kw_g[h // 2][:, h % 2 * HALF : (h % 2 + 1) * HALF]
-            nc.vector.tensor_copy(k4[h][:].bitcast(U16), words.bitcast(U16).rearrange("g (n o) -> g o n", o=PASSES))
+            nc.vector.tensor_copy(
+                k4[h][:].bitcast(U16), words.bitcast(U16).rearrange("g (j n o) -> g j o n", n=P, o=PASSES)
+            )
 
         gather_keys(0)
         gather_keys(1)
@@ -192,7 +194,7 @@ def tile_attend_pkv4q_soft_cap_kb_kernel(
                 for o in range(PASSES):
                     nc.tensor.matmul_mx(
                         out=s_t[:, j, :],
-                        lhsT=k4[h][:, o, 2 * j * P : 2 * (j + 1) * P].bitcast(FP4X4),
+                        lhsT=k4[h][:, j, o, :].bitcast(FP4X4),
                         lhsT_scale=ks_plane[:, o, h * HALF + j * P : h * HALF + (j + 1) * P],
                         rhs=qw[:, o, :].bitcast(FP8X4),
                         rhs_scale=qs[:, o, :],

@@ -53,7 +53,6 @@ def tile_attend_pkv4q_soft_cap_kb_kernel(
         ks_pool = tile("ks_pool", [P, T], U8)
         kb_pool = tile("kb_pool", [P, T], F32)
         vs_pool = tile("vs_pool", [P, T], F32)
-        vw_pool = tile("vw_pool", [P, POOL_PAGES * DV], I32)
         qw = tile("qw", [P, PASSES, NQ], I32)
         qs = tile("qs", [P, PASSES, NQ], U8)
         ks_rows = tile("ks_rows", [P, N], U8)
@@ -63,9 +62,21 @@ def tile_attend_pkv4q_soft_cap_kb_kernel(
         vsc_pool = tile("vsc_pool", [P, POOL_PAGES * DV], U8)
         vsc_rows = tile("vsc_rows", [P, PAGES * DV], U8)
         vsc_plane = tile("vsc_plane", [P, PAGES * DV], U8)
-        first = tile("first", [P, HALF + 1], F32)
-        middle = [tile("middle%d" % i, [P, PAGE], F32) for i in range(PAGES - 1)]
-        floor = first[:, HALF:]
+        expc = [tile("expc%d" % e, [P, PAGE + 8], F32) for e in range(PAGES)]
+        maxima = expc[PAGES - 1][:, PAGE:]
+        floor = maxima[:, 0:1]
+
+        def slots(first, count):
+            return offsets[:, first // 16 : (first + count) // 16]
+
+        def gather(dst, window, entries):
+            nc.vector.tensor_copy(dst, window.indirect(entries))
+
+        def gather_times(dst, window, entries, factor):
+            nc.vector.tensor_tensor(dst, window.indirect(entries), factor, ALU.mult)
+
+        def gather_on_scalar(dst, window, entries):
+            nc.scalar.activation(dst, window.indirect(entries), ACT.Copy)
 
         def page_offsets(e):
             return offsets[:, e * PAGE // 16 : (e + 1) * PAGE // 16]
@@ -97,8 +108,8 @@ def tile_attend_pkv4q_soft_cap_kb_kernel(
 
         vs_rows = tile("vs_rows", [P, SPREAD // P], F32)
         nc.scalar.dma_start(ks_pool[KS_ROW:, :].bitcast(I32), k_scales.rearrange("o f t -> f o t").bitcast(I32))
-        nc.sync.dma_start(offsets[:], offs)
         nc.sync.dma_start(vs_rows[:], vs[0, :SPREAD].rearrange("(p c) -> p c", p=P))
+        nc.sync.dma_start(offsets[:], offs)
         load_key_words(0)
         nc.sync.dma_start(
             vsc_pool[0:P:8, :].rearrange("f (u e) -> f u e", u=POOL_PAGES).bitcast(I32),
@@ -114,22 +125,23 @@ def tile_attend_pkv4q_soft_cap_kb_kernel(
         load_q_scales(2)
         load_q_scales(3)
 
-        nc.vector.tensor_copy(ks_rows[:], ks_pool[:].indirect(offsets[:]))
-        nc.vector.tensor_copy(vsc_rows[:], vsc_pool[:].indirect(voffsets[:]))
+        gather(ks_rows[:], ks_pool[:], offsets[:])
+        gather(vsc_rows[:], vsc_pool[:], voffsets[:])
         for quad in (0, 2, 1, 3):
             nc.sync.dma_start(
                 ks_plane[32 * quad : 32 * quad + 4, :, :].bitcast(I32),
                 ks_rows[KS_ROW + 8 * quad : KS_ROW + 8 * quad + 8, :].bitcast(I32),
             )
+        vw_pool = tile("vw_pool", [P, POOL_PAGES * DV], I32, tag="ks_pool")
+        nc.sync.dma_start(
+            vw_pool[:].rearrange("g (u e) -> g u e", u=POOL_PAGES),
+            v_words.rearrange("u g e r -> g u (e r)").bitcast(I32),
+        )
         for quad in range(4):
             nc.sync.dma_start(
                 vsc_plane[32 * quad : 32 * quad + 4, :].bitcast(I32),
                 vsc_rows[32 * quad : 32 * quad + 32 : 8, :].bitcast(I32),
             )
-        nc.sync.dma_start(
-            vw_pool[:].rearrange("g (u e) -> g u e", u=POOL_PAGES),
-            v_words.rearrange("u g e r -> g u (e r)").bitcast(I32),
-        )
 
         vs_view = vs_pool[:, :SPREAD].rearrange("m (n c) -> m n c", c=SPREAD // P)
         for blk in range(SPREAD // P // TILES):
@@ -141,8 +153,8 @@ def tile_attend_pkv4q_soft_cap_kb_kernel(
 
         half_kb = tile("half_kb", [P, PAGES * TILES], F32)
         kb_all = tile("kb_all", [P, N], F32)
-        nc.vector.tensor_copy(kb_all[:, :PAGE], kb_pool[:].indirect(offsets[:, : PAGE // 16]))
-        nc.vector.tensor_copy(kb_all[:, PAGE:], kb_pool[:].indirect(offsets[:, PAGE // 16 :]))
+        gather(kb_all[:, :PAGE], kb_pool[:], offsets[:, : PAGE // 16])
+        gather(kb_all[:, PAGE:], kb_pool[:], offsets[:, PAGE // 16 :])
         for e in range(PAGES):
             kb_g = kb_all[:, e * PAGE : (e + 1) * PAGE]
             kb_t = ps.tile([P, TILES, P], F32, name="kb_t%d" % e, tag="turn%d" % e)
@@ -150,31 +162,32 @@ def tile_attend_pkv4q_soft_cap_kb_kernel(
                 nc.tensor.transpose(kb_t[:, j, :], kb_g[:, j * P : (j + 1) * P], ident[:])
             nc.scalar.mul(half_kb[:, e * TILES : (e + 1) * TILES], kb_t[:, :, KB_ROW], 1.0 / CAP)
 
-        kw_g = [tile("kw_g%d" % e, [P, PAGE], U32)[:] for e in range(PAGES)]
+        vs_g = tile("vs_g", [P, N - PAGE], F32)
+        for e in range(PAGES - 1):
+            gather_on_scalar(vs_g[:, e * PAGE : (e + 1) * PAGE], vs_pool[:], slots(HALF + e * PAGE, PAGE))
+
+        kw_g = [tile("kw_g%d" % h, [P, HALF], U32) for h in range(HALVES)]
         k4 = [tile("k4_%d" % h, [P, HALF // P, PASSES, 2 * P], U8) for h in range(HALVES)]
 
-        def gather_keys(e):
-            nc.vector.tensor_copy(kw_g[e], kw_pool[:].bitcast(U32).indirect(page_offsets(e)))
+        def gather_keys(h):
+            gather(kw_g[h][:], kw_pool[:].bitcast(U32), slots(h * HALF, HALF))
 
         def part_keys(h):
-            words = kw_g[h // 2][:, h % 2 * HALF : (h % 2 + 1) * HALF]
             nc.vector.tensor_copy(
-                k4[h][:].bitcast(U16), words.bitcast(U16).rearrange("g (j n o) -> g j o n", n=P, o=PASSES)
+                k4[h][:].bitcast(U16), kw_g[h][:].bitcast(U16).rearrange("g (j n o) -> g j o n", n=P, o=PASSES)
             )
 
         gather_keys(0)
-        gather_keys(1)
-        for h in range(HALVES - 2):
+        for h in range(HALVES):
+            if h + 1 < HALVES:
+                gather_keys(h + 1)
             part_keys(h)
-        gather_keys(2)
-        part_keys(HALVES - 2)
-        part_keys(HALVES - 1)
 
-        products = tile("products", [P, N + HALF + 4], F32, tag="kw_g%d" % (PAGES - 1))
-        last = products[:, N:]
-        expc = [first[:, :HALF]]
-        expc.extend([middle[h // 2][:, h % 2 * HALF : (h % 2 + 1) * HALF] for h in range(HALVES - 2)])
-        expc.append(last[:, :HALF])
+        vw_first = tile("vw_first", [P, DV], U32, tag="kw_g%d" % (HALVES - 2))
+        gather(vw_first[:], vw_pool[:].bitcast(U32), voffsets[:, : DV // 16])
+
+        sums = tile("sums", [P, HALVES], F32)
+        early = tile("early", [P, N - HALF], F32, tag="kw_g%d" % (HALVES - 1))
 
         warm = ps.tile([P, PASSES * NQ], F32, name="warm", tag="acc")
         for width in WARM_WIDTHS:
@@ -210,48 +223,53 @@ def tile_attend_pkv4q_soft_cap_kb_kernel(
             th = ps.tile([P, 2, P], F32, name="th%d" % h, tag="turn%d" % (h % PAGES))
             for j in range(2):
                 nc.tensor.transpose(th[:, j, :], th_t[:, j, :], ident[:])
-            nc.scalar.activation(expc[h], th[:].rearrange("q j k -> q (j k)"), ACT.Exp, scale=CAP)
+            exp_h = expc[h // 2][:, h % 2 * HALF : (h % 2 + 1) * HALF]
+            nc.scalar.activation(
+                exp_h, th[:].rearrange("q j k -> q (j k)"), ACT.Exp, scale=CAP, accum_out=sums[:, h : h + 1]
+            )
+            if h == 0:
+                gather_times(early[:, :HALF], vs_pool[:], slots(0, HALF), exp_h)
+            elif h < HALVES - 1:
+                nc.gpsimd.tensor_tensor(
+                    early[:, h * HALF : (h + 1) * HALF], exp_h, vs_g[:, (h - 1) * HALF : h * HALF], ALU.mult
+                )
 
-        top = tile("top", [P, 1], F32)[:]
-        total = tile("total", [P, 1], F32)[:]
-        inv = tile("inv", [P, 1], F32)
-        inv_top = inv[:, 0:1]
-        folded = ps.tile([P, NQ], F32, name="folded", tag="turn%d" % ((HALVES - 1) % PAGES))
-        for t in range(N // P):
-            nc.tensor.matmul(
-                folded[:],
-                expc[t // 2][:, t % 2 * P : (t % 2 + 1) * P],
-                ident[:],
-                start=(t == 0),
-                stop=(t == N // P - 1),
-                is_transpose=True,
-            )
-        folded_sb = tile("folded_sb", [P, NQ], F32)
-        nc.scalar.copy(folded_sb[:], folded[:])
-        chunks = [(0, HALF, first[:]), (HALF, PAGE, middle[0][:]), (HALF + PAGE, PAGE, middle[1][:])]
-        for i, (c0, n, ex) in enumerate(chunks):
-            nc.vector.tensor_reduce(last[:, HALF + i : HALF + i + 1], ex, AX.X, ALU.max)
-            nc.vector.tensor_tensor(
-                products[:, c0 : c0 + n], vs_pool[:].indirect(offsets[:, c0 // 16 : (c0 + n) // 16]), ex[:, :n], ALU.mult
-            )
-        nc.vector.tensor_reduce(top, last[:, : HALF + len(chunks)], AX.X, ALU.max)
-        nc.vector.tensor_tensor(
-            products[:, N - HALF : N], vs_pool[:].indirect(offsets[:, (N - HALF) // 16 :]), last[:, :HALF], ALU.mult
-        )
+        top = tile("top", [P, 1], F32, tag="late")[:]
+        inv_top = tile("inv_top", [P, 1], F32)[:]
+        last = expc[PAGES - 1]
+        nc.vector.tensor_reduce(maxima[:, 1:2], expc[0][:, :PAGE], AX.X, ALU.max)
+        for h in range(2, HALVES - 1):
+            exp_h = expc[h // 2][:, h % 2 * HALF : (h % 2 + 1) * HALF]
+            nc.vector.tensor_reduce(maxima[:, h : h + 1], exp_h, AX.X, ALU.max)
+        nc.vector.tensor_reduce(top, last[:, HALF : PAGE + HALVES - 1], AX.X, ALU.max)
         nc.vector.reciprocal(inv_top, top)
+
+        def dealt(products):
+            return products.rearrange("q (g u c) -> q u g c", u=2, c=2)
 
         words = []
         for e in range(PAGES):
             wb = tile("wb%d" % e, [P, 2, P, 2], BF16)
-            source = products[:, e * PAGE : (e + 1) * PAGE].rearrange("q (g u c) -> q u g c", u=2, c=2)
-            if e == 1:
-                nc.scalar.activation(wb[:], source, ACT.Copy, scale=inv_top)
+            if e == 0:
+                nc.scalar.activation(wb[:], dealt(early[:, :PAGE]), ACT.Copy, scale=inv_top)
+            elif e < PAGES - 1:
+                nc.vector.tensor_scalar_mul(wb[:], dealt(early[:, e * PAGE : (e + 1) * PAGE]), inv_top)
             else:
-                nc.vector.tensor_scalar_mul(wb[:], source, inv_top)
+                late = tile("late", [P, HALF], F32)
+                gather_times(late[:], vs_pool[:], slots(N - HALF, HALF), last[:, HALF:PAGE])
+                nc.vector.tensor_scalar_mul(wb[:, :, : P // 2, :], dealt(early[:, e * PAGE :]), inv_top)
+                nc.vector.tensor_scalar_mul(wb[:, :, P // 2 :, :], dealt(late[:]), inv_top)
             words.append(wb[:].rearrange("q u g c -> q u (g c)").bitcast(F32))
 
-        vw_g = tile("vw_g", [P, PAGES * DV], U32, tag="kw_g%d" % (PAGES - 1))
-        nc.vector.tensor_copy(vw_g[:], vw_pool[:].bitcast(U32).indirect(voffsets[:]))
+        vw_rest = tile("vw_rest", [P, (PAGES - 1) * DV], U32, tag="kw_g%d" % (HALVES - 1))
+        gather(vw_rest[:], vw_pool[:].bitcast(U32), voffsets[:, DV // 16 :])
+        vw_g = [vw_first[:]] + [vw_rest[:, e * DV : (e + 1) * DV] for e in range(PAGES - 1)]
+
+        total = tile("total", [P, 1], F32)[:]
+        scaled_sums = tile("scaled_sums", [P, HALVES], F32)
+        nc.vector.tensor_scalar(scaled_sums[:], sums[:], inv_top, None, ALU.mult, ALU.add, accum_out=total)
+        inv_total = tile("inv_total", [P, 1], F32)[:]
+        nc.vector.reciprocal(inv_total, total)
 
         acc = ps.tile([P, DV], F32, name="acc", tag="acc")
         for e in range(PAGES):
@@ -269,18 +287,12 @@ def tile_attend_pkv4q_soft_cap_kb_kernel(
                 out=acc[:],
                 lhsT=codes[:].bitcast(FP8X4),
                 lhsT_scale=scales[:],
-                rhs=vw_g[:, e * DV : (e + 1) * DV].bitcast(FP8X4),
+                rhs=vw_g[e].bitcast(FP8X4),
                 rhs_scale=vsc_plane[:, e * DV : (e + 1) * DV],
                 start=(e == 0),
                 stop=(e == PAGES - 1),
             )
 
-        unfolded = ps.tile([P, P], F32, name="unfolded", tag="score0")
-        nc.tensor.transpose(unfolded[:], folded_sb[:], ident[:])
-        sums_copy = tile("sums_copy", [P, P], F32)
-        nc.scalar.activation(sums_copy[:], unfolded[:], ACT.Copy, accum_out=total)
-        inv_total = tile("inv_total", [P, 1], F32)[:]
-        nc.vector.reciprocal(inv_total, total)
         result = tile("result", [P, DV], F32)
-        nc.vector.tensor_scalar(result[:], acc[:], inv_total, top, ALU.mult, ALU.mult)
+        nc.vector.tensor_scalar_mul(result[:], acc[:], inv_total)
         nc.sync.dma_start(out[0], result[:])

@@ -15,6 +15,7 @@ KB_ROW = P - 1
 HALF = PAGE // 2
 HALVES = N // HALF
 SCORE_BANKS = 3
+BANKS = 3
 KW_CUTS = (0, 3 * T // 16, T // 2, T)
 KS_ROW = 96
 WARM_WIDTHS = (256, 256, 256, 128)
@@ -62,8 +63,7 @@ def tile_attend_pkv4q_soft_cap_kb_kernel(
         vsc_pool = tile("vsc_pool", [P, POOL_PAGES * DV], U8)
         vsc_rows = tile("vsc_rows", [P, PAGES * DV], U8)
         vsc_plane = tile("vsc_plane", [P, PAGES * DV], U8)
-        expc = [tile("expc%d" % e, [P, PAGE + 8], F32) for e in range(PAGES)]
-        maxima = expc[PAGES - 1][:, PAGE:]
+        maxima = tile("maxima", [P, HALVES + 1], F32, tag="late")
         floor = maxima[:, 0:1]
 
         def slots(first, count):
@@ -97,10 +97,10 @@ def tile_attend_pkv4q_soft_cap_kb_kernel(
         make_identity(nc, ident[:])
         nc.gpsimd.memset(kb_pool[:KB_ROW, :KB_FIRST].bitcast(I32), 0)
         nc.gpsimd.memset(kb_pool[:KB_ROW, KB_FIRST:].bitcast(I32), 0)
-        nc.vector.memset(floor, -CAP)
+        nc.vector.memset(floor, -16.0)
         zero_words(vsc_pool[:].bitcast(I32))
         zero_words(ks_pool[:KS_ROW, :].bitcast(I32))
-        nc.scalar.activation(floor, floor, ACT.Exp)
+        nc.scalar.activation(floor, floor, ACT.Tanh)
 
         def load_key_words(piece):
             cols = slice(KW_CUTS[piece], KW_CUTS[piece + 1])
@@ -163,8 +163,7 @@ def tile_attend_pkv4q_soft_cap_kb_kernel(
             nc.scalar.mul(half_kb[:, e * TILES : (e + 1) * TILES], kb_t[:, :, KB_ROW], 1.0 / CAP)
 
         vs_g = tile("vs_g", [P, N - PAGE], F32)
-        for e in range(PAGES - 1):
-            gather_on_scalar(vs_g[:, e * PAGE : (e + 1) * PAGE], vs_pool[:], slots(HALF + e * PAGE, PAGE))
+        gather_on_scalar(vs_g[:], vs_pool[:], slots(0, N - PAGE))
 
         kw_g = [tile("kw_g%d" % h, [P, HALF], U32) for h in range(HALVES)]
         k4 = [tile("k4_%d" % h, [P, HALF // P, PASSES, 2 * P], U8) for h in range(HALVES)]
@@ -183,11 +182,7 @@ def tile_attend_pkv4q_soft_cap_kb_kernel(
                 gather_keys(h + 1)
             part_keys(h)
 
-        vw_first = tile("vw_first", [P, DV], U32, tag="kw_g%d" % (HALVES - 2))
-        gather(vw_first[:], vw_pool[:].bitcast(U32), voffsets[:, : DV // 16])
-
-        sums = tile("sums", [P, HALVES], F32)
-        early = tile("early", [P, N - HALF], F32, tag="kw_g%d" % (HALVES - 1))
+        early = tile("early", [P, N - PAGE], F32, tag="kw_g%d" % (HALVES - 1))
 
         warm = ps.tile([P, PASSES * NQ], F32, name="warm", tag="acc")
         for width in WARM_WIDTHS:
@@ -200,6 +195,17 @@ def tile_attend_pkv4q_soft_cap_kb_kernel(
                 start=True,
                 stop=True,
             )
+
+        expc = []
+        turned = []
+
+        def exponentials(h):
+            exp_h = tile("expc%d" % h, [P, HALF], F32, tag="half_kb" if h == BANKS else None)[:]
+            expc.append(exp_h)
+            nc.scalar.activation(exp_h, turned[h], ACT.Exp, scale=CAP)
+            if h < HALVES - 2:
+                cols = slice(h * HALF, (h + 1) * HALF)
+                nc.gpsimd.tensor_tensor(early[:, cols], exp_h, vs_g[:, cols], ALU.mult)
 
         for h in range(HALVES):
             s_t = ps.tile([P, 2, NQ], F32, name="s_t%d" % h, tag="score%d" % (h % SCORE_BANKS))
@@ -220,60 +226,60 @@ def tile_attend_pkv4q_soft_cap_kb_kernel(
                 nc.scalar.activation(
                     th_t[:, j, :], s_t[:, j, :], ACT.Tanh, bias=half_kb[:, col : col + 1], scale=1.0 / CAP
                 )
-            th = ps.tile([P, 2, P], F32, name="th%d" % h, tag="turn%d" % (h % PAGES))
+            th = ps.tile([P, 2, P], F32, name="th%d" % h, tag=("turn0", "turn1", "turn2", "spare")[h % 4])
             for j in range(2):
                 nc.tensor.transpose(th[:, j, :], th_t[:, j, :], ident[:])
-            exp_h = expc[h // 2][:, h % 2 * HALF : (h % 2 + 1) * HALF]
-            nc.scalar.activation(
-                exp_h, th[:].rearrange("q j k -> q (j k)"), ACT.Exp, scale=CAP, accum_out=sums[:, h : h + 1]
-            )
-            if h == 0:
-                gather_times(early[:, :HALF], vs_pool[:], slots(0, HALF), exp_h)
-            elif h < HALVES - 1:
-                nc.gpsimd.tensor_tensor(
-                    early[:, h * HALF : (h + 1) * HALF], exp_h, vs_g[:, (h - 1) * HALF : h * HALF], ALU.mult
-                )
+            turned.append(th[:].rearrange("q j k -> q (j k)"))
+            if h < BANKS:
+                exponentials(h)
+            nc.vector.tensor_reduce(maxima[:, h + 1 : h + 2], turned[h], AX.X, ALU.max)
+        for h in range(BANKS, HALVES):
+            exponentials(h)
 
-        top = tile("top", [P, 1], F32, tag="late")[:]
+        top = tile("top", [P, 1], F32)[:]
         inv_top = tile("inv_top", [P, 1], F32)[:]
-        last = expc[PAGES - 1]
-        nc.vector.tensor_reduce(maxima[:, 1:2], expc[0][:, :PAGE], AX.X, ALU.max)
-        for h in range(2, HALVES - 1):
-            exp_h = expc[h // 2][:, h % 2 * HALF : (h % 2 + 1) * HALF]
-            nc.vector.tensor_reduce(maxima[:, h : h + 1], exp_h, AX.X, ALU.max)
-        nc.vector.tensor_reduce(top, last[:, HALF : PAGE + HALVES - 1], AX.X, ALU.max)
-        nc.vector.reciprocal(inv_top, top)
+        nc.vector.tensor_reduce(top, maxima[:], AX.X, ALU.max)
+        nc.scalar.activation(inv_top, top, ACT.Exp, scale=-CAP)
+        late = tile("late", [P, PAGE], F32)
+
+        def late_product(h):
+            cols = slice(h % 2 * HALF, (h % 2 + 1) * HALF)
+            gather_times(late[:, cols], vs_pool[:], slots(h * HALF, HALF), expc[h])
 
         def dealt(products):
             return products.rearrange("q (g u c) -> q u g c", u=2, c=2)
 
-        words = []
-        for e in range(PAGES):
-            wb = tile("wb%d" % e, [P, 2, P, 2], BF16)
-            if e == 0:
-                nc.scalar.activation(wb[:], dealt(early[:, :PAGE]), ACT.Copy, scale=inv_top)
-            elif e < PAGES - 1:
-                nc.vector.tensor_scalar_mul(wb[:], dealt(early[:, e * PAGE : (e + 1) * PAGE]), inv_top)
-            else:
-                late = tile("late", [P, HALF], F32)
-                gather_times(late[:], vs_pool[:], slots(N - HALF, HALF), last[:, HALF:PAGE])
-                nc.vector.tensor_scalar_mul(wb[:, :, : P // 2, :], dealt(early[:, e * PAGE :]), inv_top)
-                nc.vector.tensor_scalar_mul(wb[:, :, P // 2 :, :], dealt(late[:]), inv_top)
-            words.append(wb[:].rearrange("q u g c -> q u (g c)").bitcast(F32))
+        folded = ps.tile([P, NQ], F32, name="folded", tag="score%d" % ((HALVES - 1) % SCORE_BANKS))
+        for t in range(N // P):
+            nc.tensor.matmul(
+                folded[:],
+                expc[t // 2][:, t % 2 * P : (t % 2 + 1) * P],
+                ident[:],
+                start=(t == 0),
+                stop=(t == N // P - 1),
+                is_transpose=True,
+            )
 
-        vw_rest = tile("vw_rest", [P, (PAGES - 1) * DV], U32, tag="kw_g%d" % (HALVES - 1))
+        wb = [tile("wb%d" % e, [P, 2, P, 2], BF16) for e in range(PAGES)]
+        nc.scalar.activation(wb[0][:], dealt(early[:, :PAGE]), ACT.Copy, scale=inv_top)
+        late_product(HALVES - 2)
+        nc.vector.tensor_scalar_mul(wb[1][:], dealt(early[:, PAGE:]), inv_top)
+        late_product(HALVES - 1)
+        vw_first = tile("vw_first", [P, DV], U32, tag="kw_g%d" % (HALVES - 1))
+        gather(vw_first[:], vw_pool[:].bitcast(U32), voffsets[:, : DV // 16])
+        nc.vector.tensor_scalar_mul(wb[2][:], dealt(late[:]), inv_top)
+        words = [w[:].rearrange("q u g c -> q u (g c)").bitcast(F32) for w in wb]
+        folded_sb = tile("folded_sb", [P, NQ], F32)
+        nc.scalar.copy(folded_sb[:], folded[:])
+
+        vw_rest = tile("vw_rest", [P, (PAGES - 1) * DV], U32, tag="late")
         gather(vw_rest[:], vw_pool[:].bitcast(U32), voffsets[:, DV // 16 :])
         vw_g = [vw_first[:]] + [vw_rest[:, e * DV : (e + 1) * DV] for e in range(PAGES - 1)]
 
-        total = tile("total", [P, 1], F32)[:]
-        scaled_sums = tile("scaled_sums", [P, HALVES], F32)
-        nc.vector.tensor_scalar(scaled_sums[:], sums[:], inv_top, None, ALU.mult, ALU.add, accum_out=total)
-        inv_total = tile("inv_total", [P, 1], F32)[:]
-        nc.vector.reciprocal(inv_total, total)
-
         acc = ps.tile([P, DV], F32, name="acc", tag="acc")
-        for e in range(PAGES):
-            w_t = ps.tile([P, 2, NQ], F32, name="w_t%d" % e, tag="score%d" % e)
+        order = (1, 0, 2)
+        for e in order:
+            w_t = ps.tile([P, 2, NQ], F32, name="w_t%d" % e, tag=("score0", "score1", "spare")[e])
             for u in range(2):
                 nc.tensor.transpose(w_t[:, u, :], words[e][:, u, :], ident[:])
             wq = tile("wq%d" % e, [P, 4 * NQ], BF16)
@@ -289,10 +295,17 @@ def tile_attend_pkv4q_soft_cap_kb_kernel(
                 lhsT_scale=scales[:],
                 rhs=vw_g[e].bitcast(FP8X4),
                 rhs_scale=vsc_plane[:, e * DV : (e + 1) * DV],
-                start=(e == 0),
-                stop=(e == PAGES - 1),
+                start=(e == order[0]),
+                stop=(e == order[-1]),
             )
 
+        unfolded = ps.tile([P, P], F32, name="unfolded", tag="score1")
+        nc.tensor.transpose(unfolded[:], folded_sb[:], ident[:])
+        sums_copy = tile("sums_copy", [P, P], F32)
+        total = tile("total", [P, 1], F32)[:]
+        nc.scalar.activation(sums_copy[:], unfolded[:], ACT.Copy, scale=inv_top, accum_out=total)
+        inv_total = tile("inv_total", [P, 1], F32)[:]
+        nc.vector.reciprocal(inv_total, total)
         result = tile("result", [P, DV], F32)
         nc.vector.tensor_scalar_mul(result[:], acc[:], inv_total)
         nc.sync.dma_start(out[0], result[:])

@@ -21,6 +21,7 @@ KS_ROW = 96
 WARM_WIDTHS = (256, 256, 256, 128)
 KB_FIRST = 256
 SPREAD = T
+EARLY = 3 * HALF
 
 FLOPS = 2 * NQ * N * (D + DV)
 
@@ -162,8 +163,8 @@ def tile_attend_pkv4q_soft_cap_kb_kernel(
                 nc.tensor.transpose(kb_t[:, j, :], kb_g[:, j * P : (j + 1) * P], ident[:])
             nc.scalar.mul(half_kb[:, e * TILES : (e + 1) * TILES], kb_t[:, :, KB_ROW], 1.0 / CAP)
 
-        vs_g = tile("vs_g", [P, N - PAGE], F32)
-        gather_on_scalar(vs_g[:], vs_pool[:], slots(0, N - PAGE))
+        vs_g = tile("vs_g", [P, EARLY], F32)
+        gather_on_scalar(vs_g[:], vs_pool[:], slots(0, EARLY))
 
         kw_g = [tile("kw_g%d" % h, [P, HALF], U32) for h in range(HALVES)]
         k4 = [tile("k4_%d" % h, [P, HALF // P, PASSES, 2 * P], U8) for h in range(HALVES)]
@@ -182,7 +183,7 @@ def tile_attend_pkv4q_soft_cap_kb_kernel(
                 gather_keys(h + 1)
             part_keys(h)
 
-        early = tile("early", [P, N - PAGE], F32, tag="kw_g%d" % (HALVES - 1))
+        early = tile("early", [P, EARLY], F32, tag="kw_g%d" % (HALVES - 1))
 
         warm = ps.tile([P, PASSES * NQ], F32, name="warm", tag="acc")
         for width in WARM_WIDTHS:
@@ -203,7 +204,7 @@ def tile_attend_pkv4q_soft_cap_kb_kernel(
             exp_h = tile("expc%d" % h, [P, HALF], F32, tag="half_kb" if h == BANKS else None)[:]
             expc.append(exp_h)
             nc.scalar.activation(exp_h, turned[h], ACT.Exp, scale=CAP)
-            if h < HALVES - 2:
+            if h < BANKS:
                 cols = slice(h * HALF, (h + 1) * HALF)
                 nc.gpsimd.tensor_tensor(early[:, cols], exp_h, vs_g[:, cols], ALU.mult)
 
@@ -240,10 +241,9 @@ def tile_attend_pkv4q_soft_cap_kb_kernel(
         inv_top = tile("inv_top", [P, 1], F32)[:]
         nc.vector.tensor_reduce(top, maxima[:], AX.X, ALU.max)
         nc.scalar.activation(inv_top, top, ACT.Exp, scale=-CAP)
-        late = tile("late", [P, PAGE], F32)
-
-        def late_product(h):
-            cols = slice(h % 2 * HALF, (h % 2 + 1) * HALF)
+        late = tile("late", [P, N - EARLY], F32)
+        for h in range(BANKS, HALVES):
+            cols = slice(h * HALF - EARLY, (h + 1) * HALF - EARLY)
             gather_times(late[:, cols], vs_pool[:], slots(h * HALF, HALF), expc[h])
 
         def dealt(products):
@@ -262,22 +262,18 @@ def tile_attend_pkv4q_soft_cap_kb_kernel(
 
         wb = [tile("wb%d" % e, [P, 2, P, 2], BF16) for e in range(PAGES)]
         nc.scalar.activation(wb[0][:], dealt(early[:, :PAGE]), ACT.Copy, scale=inv_top)
-        late_product(HALVES - 2)
-        nc.vector.tensor_scalar_mul(wb[1][:], dealt(early[:, PAGE:]), inv_top)
-        late_product(HALVES - 1)
-        vw_first = tile("vw_first", [P, DV], U32, tag="kw_g%d" % (HALVES - 1))
-        gather(vw_first[:], vw_pool[:].bitcast(U32), voffsets[:, : DV // 16])
-        nc.vector.tensor_scalar_mul(wb[2][:], dealt(late[:]), inv_top)
+        nc.vector.tensor_scalar_mul(wb[1][:, :, : P // 2, :], dealt(early[:, PAGE:]), inv_top)
+        nc.vector.tensor_scalar_mul(wb[1][:, :, P // 2 :, :], dealt(late[:, :HALF]), inv_top)
+        nc.vector.tensor_scalar_mul(wb[2][:], dealt(late[:, HALF:]), inv_top)
         words = [w[:].rearrange("q u g c -> q u (g c)").bitcast(F32) for w in wb]
         folded_sb = tile("folded_sb", [P, NQ], F32)
         nc.scalar.copy(folded_sb[:], folded[:])
 
-        vw_rest = tile("vw_rest", [P, (PAGES - 1) * DV], U32, tag="late")
-        gather(vw_rest[:], vw_pool[:].bitcast(U32), voffsets[:, DV // 16 :])
-        vw_g = [vw_first[:]] + [vw_rest[:, e * DV : (e + 1) * DV] for e in range(PAGES - 1)]
+        vw_g = tile("vw_g", [P, PAGES * DV], U32, tag="kw_g%d" % (HALVES - 1))
+        gather(vw_g[:], vw_pool[:].bitcast(U32), voffsets[:])
 
         acc = ps.tile([P, DV], F32, name="acc", tag="acc")
-        order = (1, 0, 2)
+        order = (0, 1, 2)
         for e in order:
             w_t = ps.tile([P, 2, NQ], F32, name="w_t%d" % e, tag=("score0", "score1", "spare")[e])
             for u in range(2):
@@ -293,13 +289,13 @@ def tile_attend_pkv4q_soft_cap_kb_kernel(
                 out=acc[:],
                 lhsT=codes[:].bitcast(FP8X4),
                 lhsT_scale=scales[:],
-                rhs=vw_g[e].bitcast(FP8X4),
+                rhs=vw_g[:, e * DV : (e + 1) * DV].bitcast(FP8X4),
                 rhs_scale=vsc_plane[:, e * DV : (e + 1) * DV],
                 start=(e == order[0]),
                 stop=(e == order[-1]),
             )
 
-        unfolded = ps.tile([P, P], F32, name="unfolded", tag="score1")
+        unfolded = ps.tile([P, P], F32, name="unfolded", tag="score0")
         nc.tensor.transpose(unfolded[:], folded_sb[:], ident[:])
         sums_copy = tile("sums_copy", [P, P], F32)
         total = tile("total", [P, 1], F32)[:]

from contextlib import ExitStack

import concourse.mybir as mybir
from concourse.masks import make_identity

N, T, D, DV, NQ = 1536, 4096, 1024, 256, 128
PAGE = 512
PAGES = N // PAGE
POOL_PAGES = T // PAGE
P = 128
PASSES = D // 512
TILES = PAGE // P
CAP = 2.0
KB_ROW = P - 1
HALF = PAGE // 2
HALVES = N // HALF
SCORE_BANKS = 3
BANKS = 3
KW_CUTS = (0, 3 * T // 16, T // 2, T)
KS_ROW = 96
WARM_WIDTHS = (256, 256, 256, 128)
KB_FIRST = 256
SPREAD = T
EARLY = 3 * HALF

FLOPS = 2 * NQ * N * (D + DV)

F32 = mybir.dt.float32
BF16 = mybir.dt.bfloat16
I32 = mybir.dt.int32
U32 = mybir.dt.uint32
U16 = mybir.dt.uint16
U8 = mybir.dt.uint8
FP8X4 = mybir.dt.float8_e4m3fn_x4
FP4X4 = mybir.dt.float4_e2m1fn_x4
ACT = mybir.ActivationFunctionType
ALU = mybir.AluOpType
AX = mybir.AxisListType


def tile_attend_pkv4q_soft_cap_kb_kernel(
    tc, q_words, q_scales, k_words, k_scales, v_words, v_scales, vs, kb, offs, voffs, out
):
    nc = tc.nc
    with ExitStack() as ctx:
        sb = ctx.enter_context(tc.tile_pool(name="sb", bufs=1))
        ps = ctx.enter_context(tc.psum_pool(name="ps", bufs=1))

        def tile(name, shape, dtype, tag=None):
            return sb.tile(shape, dtype, name=name, tag=tag or name, align_bytes=64)

        offsets = sb.tile([P, N // 16], U16, name="offsets")
        voffsets = sb.tile([P, PAGES * DV // 16], U16, name="voffsets")
        kw_pool = tile("kw_pool", [P, T], I32)
        ks_pool = tile("ks_pool", [P, T], U8)
        kb_pool = tile("kb_pool", [P, T], F32)
        vs_pool = tile("vs_pool", [P, T], F32)
        qw = tile("qw", [P, PASSES, NQ], I32)
        qs = tile("qs", [P, PASSES, NQ], U8)
        ks_rows = tile("ks_rows", [P, N], U8)
        ks_plane = tile("ks_plane", [P, PASSES, N], U8)
        ident = tile("ident", [P, P], F32)

        vsc_pool = tile("vsc_pool", [P, POOL_PAGES * DV], U8)
        vsc_rows = tile("vsc_rows", [P, PAGES * DV], U8)
        vsc_plane = tile("vsc_plane", [P, PAGES * DV], U8)
        maxima = tile("maxima", [P, HALVES + 1], F32, tag="late")
        floor = maxima[:, 0:1]

        def slots(first, count):
            return offsets[:, first // 16 : (first + count) // 16]

        def gather(dst, window, entries):
            nc.vector.tensor_copy(dst, window.indirect(entries))

        def gather_times(dst, window, entries, factor):
            nc.vector.tensor_tensor(dst, window.indirect(entries), factor, ALU.mult)

        def gather_on_scalar(dst, window, entries):
            nc.scalar.activation(dst, window.indirect(entries), ACT.Copy)

        def page_offsets(e):
            return offsets[:, e * PAGE // 16 : (e + 1) * PAGE // 16]

        kw_flat = k_words[0].rearrange("g t b -> g (t b)").bitcast(I32)

        def load_q_scales(quad):
            nc.sync.dma_start(
                qs[32 * quad : 32 * quad + 4, :, :].bitcast(I32),
                q_scales[0, :, 4 * quad : 4 * quad + 4, :].rearrange("o r q -> r o q").bitcast(I32),
            )

        def zero_words(words):
            half = words.shape[1] // 2 + 1
            nc.vector.memset(words[:, :half], 0)
            nc.vector.memset(words[:, half:], 0)

        make_identity(nc, ident[:])
        nc.gpsimd.memset(kb_pool[:KB_ROW, :KB_FIRST].bitcast(I32), 0)
        nc.gpsimd.memset(kb_pool[:KB_ROW, KB_FIRST:].bitcast(I32), 0)
        nc.vector.memset(floor, -16.0)
        zero_words(vsc_pool[:].bitcast(I32))
        zero_words(ks_pool[:KS_ROW, :].bitcast(I32))
        nc.scalar.activation(floor, floor, ACT.Tanh)

        def load_key_words(piece):
            cols = slice(KW_CUTS[piece], KW_CUTS[piece + 1])
            nc.sync.dma_start(kw_pool[:, cols], kw_flat[:, cols])

        vs_rows = tile("vs_rows", [P, SPREAD // P], F32)
        nc.scalar.dma_start(ks_pool[KS_ROW:, :].bitcast(I32), k_scales.rearrange("o f t -> f o t").bitcast(I32))
        nc.sync.dma_start(vs_rows[:], vs[0, :SPREAD].rearrange("(p c) -> p c", p=P))
        nc.sync.dma_start(offsets[:], offs)
        load_key_words(0)
        nc.sync.dma_start(
            vsc_pool[0:P:8, :].rearrange("f (u e) -> f u e", u=POOL_PAGES).bitcast(I32),
            v_scales.rearrange("u f e -> f u e").bitcast(I32),
        )
        nc.sync.dma_start(voffsets[:], voffs)
        nc.sync.dma_start(kb_pool[KB_ROW : KB_ROW + 1, :], kb[0:1, :])
        load_key_words(1)
        load_q_scales(0)
        load_q_scales(1)
        load_key_words(2)
        nc.sync.dma_start(qw[:], q_words[0].rearrange("o g q r -> g o (q r)").bitcast(I32))
        load_q_scales(2)
        load_q_scales(3)

        gather(ks_rows[:], ks_pool[:], offsets[:])
        gather(vsc_rows[:], vsc_pool[:], voffsets[:])
        for quad in (0, 2, 1, 3):
            nc.sync.dma_start(
                ks_plane[32 * quad : 32 * quad + 4, :, :].bitcast(I32),
                ks_rows[KS_ROW + 8 * quad : KS_ROW + 8 * quad + 8, :].bitcast(I32),
            )
        vw_pool = tile("vw_pool", [P, POOL_PAGES * DV], I32, tag="ks_pool")
        nc.sync.dma_start(
            vw_pool[:].rearrange("g (u e) -> g u e", u=POOL_PAGES),
            v_words.rearrange("u g e r -> g u (e r)").bitcast(I32),
        )
        for quad in range(4):
            nc.sync.dma_start(
                vsc_plane[32 * quad : 32 * quad + 4, :].bitcast(I32),
                vsc_rows[32 * quad : 32 * quad + 32 : 8, :].bitcast(I32),
            )

        vs_view = vs_pool[:, :SPREAD].rearrange("m (n c) -> m n c", c=SPREAD // P)
        for blk in range(SPREAD // P // TILES):
            spread = ps.tile([P, TILES, P], F32, name="spread%d" % blk, tag="score%d" % (blk % PAGES))
            for j in range(TILES):
                c = blk * TILES + j
                nc.tensor.transpose(spread[:, j, :], vs_rows[:, c : c + 1].to_broadcast([P, P]), ident[:])
            nc.scalar.copy(vs_view[:, :, blk * TILES : (blk + 1) * TILES], spread[:].rearrange("m j n -> m n j"))

        half_kb = tile("half_kb", [P, PAGES * TILES], F32)
        kb_all = tile("kb_all", [P, N], F32)
        gather(kb_all[:, :PAGE], kb_pool[:], offsets[:, : PAGE // 16])
        gather(kb_all[:, PAGE:], kb_pool[:], offsets[:, PAGE // 16 :])
        for e in range(PAGES):
            kb_g = kb_all[:, e * PAGE : (e + 1) * PAGE]
            kb_t = ps.tile([P, TILES, P], F32, name="kb_t%d" % e, tag="turn%d" % e)
            for j in range(TILES):
                nc.tensor.transpose(kb_t[:, j, :], kb_g[:, j * P : (j + 1) * P], ident[:])
            nc.scalar.mul(half_kb[:, e * TILES : (e + 1) * TILES], kb_t[:, :, KB_ROW], 1.0 / CAP)

        vs_g = tile("vs_g", [P, EARLY], F32)
        gather_on_scalar(vs_g[:], vs_pool[:], slots(0, EARLY))

        kw_g = [tile("kw_g%d" % h, [P, HALF], U32) for h in range(HALVES)]
        k4 = [tile("k4_%d" % h, [P, HALF // P, PASSES, 2 * P], U8) for h in range(HALVES)]

        def gather_keys(h):
            gather(kw_g[h][:], kw_pool[:].bitcast(U32), slots(h * HALF, HALF))

        def part_keys(h):
            nc.vector.tensor_copy(
                k4[h][:].bitcast(U16), kw_g[h][:].bitcast(U16).rearrange("g (j n o) -> g j o n", n=P, o=PASSES)
            )

        gather_keys(0)
        for h in range(HALVES):
            if h + 1 < HALVES:
                gather_keys(h + 1)
            part_keys(h)

        early = tile("early", [P, EARLY], F32, tag="kw_g%d" % (HALVES - 1))

        warm = ps.tile([P, PASSES * NQ], F32, name="warm", tag="acc")
        for width in WARM_WIDTHS:
            nc.tensor.matmul_mx(
                out=warm[:, :width],
                lhsT=qw[:, 0, :].bitcast(FP8X4),
                lhsT_scale=qs[:, 0, :],
                rhs=qw[:].rearrange("g o q -> g (o q)")[:, :width].bitcast(FP8X4),
                rhs_scale=qs[:].rearrange("g o q -> g (o q)")[:, :width],
                start=True,
                stop=True,
            )

        expc = []
        turned = []

        def exponentials(h):
            exp_h = tile("expc%d" % h, [P, HALF], F32, tag="half_kb" if h == BANKS else None)[:]
            expc.append(exp_h)
            nc.scalar.activation(exp_h, turned[h], ACT.Exp, scale=CAP)
            if h < BANKS:
                cols = slice(h * HALF, (h + 1) * HALF)
                nc.gpsimd.tensor_tensor(early[:, cols], exp_h, vs_g[:, cols], ALU.mult)

        for h in range(HALVES):
            s_t = ps.tile([P, 2, NQ], F32, name="s_t%d" % h, tag="score%d" % (h % SCORE_BANKS))
            for j in range(2):
                for o in range(PASSES):
                    nc.tensor.matmul_mx(
                        out=s_t[:, j, :],
                        lhsT=k4[h][:, j, o, :].bitcast(FP4X4),
                        lhsT_scale=ks_plane[:, o, h * HALF + j * P : h * HALF + (j + 1) * P],
                        rhs=qw[:, o, :].bitcast(FP8X4),
                        rhs_scale=qs[:, o, :],
                        start=(o == 0),
                        stop=(o == PASSES - 1),
                    )
            th_t = tile("th_t%d" % h, [P, 2, NQ], F32)
            for j in range(2):
                col = 2 * h + j
                nc.scalar.activation(
                    th_t[:, j, :], s_t[:, j, :], ACT.Tanh, bias=half_kb[:, col : col + 1], scale=1.0 / CAP
                )
            th = ps.tile([P, 2, P], F32, name="th%d" % h, tag=("turn0", "turn1", "turn2", "spare")[h % 4])
            for j in range(2):
                nc.tensor.transpose(th[:, j, :], th_t[:, j, :], ident[:])
            turned.append(th[:].rearrange("q j k -> q (j k)"))
            if h < BANKS:
                exponentials(h)
            nc.vector.tensor_reduce(maxima[:, h + 1 : h + 2], turned[h], AX.X, ALU.max)
        for h in range(BANKS, HALVES):
            exponentials(h)

        top = tile("top", [P, 1], F32)[:]
        inv_top = tile("inv_top", [P, 1], F32)[:]
        nc.vector.tensor_reduce(top, maxima[:], AX.X, ALU.max)
        nc.scalar.activation(inv_top, top, ACT.Exp, scale=-CAP)
        late = tile("late", [P, N - EARLY], F32)
        for h in range(BANKS, HALVES):
            cols = slice(h * HALF - EARLY, (h + 1) * HALF - EARLY)
            gather_times(late[:, cols], vs_pool[:], slots(h * HALF, HALF), expc[h])

        def dealt(products):
            return products.rearrange("q (g u c) -> q u g c", u=2, c=2)

        folded = ps.tile([P, NQ], F32, name="folded", tag="score%d" % ((HALVES - 1) % SCORE_BANKS))
        for t in range(N // P):
            nc.tensor.matmul(
                folded[:],
                expc[t // 2][:, t % 2 * P : (t % 2 + 1) * P],
                ident[:],
                start=(t == 0),
                stop=(t == N // P - 1),
                is_transpose=True,
            )

        wb = [tile("wb%d" % e, [P, 2, P, 2], BF16) for e in range(PAGES)]
        nc.scalar.activation(wb[0][:], dealt(early[:, :PAGE]), ACT.Copy, scale=inv_top)
        nc.vector.tensor_scalar_mul(wb[1][:, :, : P // 2, :], dealt(early[:, PAGE:]), inv_top)
        nc.vector.tensor_scalar_mul(wb[1][:, :, P // 2 :, :], dealt(late[:, :HALF]), inv_top)
        nc.vector.tensor_scalar_mul(wb[2][:], dealt(late[:, HALF:]), inv_top)
        words = [w[:].rearrange("q u g c -> q u (g c)").bitcast(F32) for w in wb]
        folded_sb = tile("folded_sb", [P, NQ], F32)
        nc.scalar.copy(folded_sb[:], folded[:])

        vw_g = tile("vw_g", [P, PAGES * DV], U32, tag="kw_g%d" % (HALVES - 1))
        gather(vw_g[:], vw_pool[:].bitcast(U32), voffsets[:])

        acc = ps.tile([P, DV], F32, name="acc", tag="acc")
        order = (0, 1, 2)
        for e in order:
            w_t = ps.tile([P, 2, NQ], F32, name="w_t%d" % e, tag=("score0", "score1", "spare")[e])
            for u in range(2):
                nc.tensor.transpose(w_t[:, u, :], words[e][:, u, :], ident[:])
            wq = tile("wq%d" % e, [P, 4 * NQ], BF16)
            nc.scalar.copy(
                wq[:].bitcast(F32).rearrange("g (q u) -> g q u", u=2), w_t[:].rearrange("g u q -> g q u")
            )
            codes = tile("codes%d" % e, [P, NQ], U32)
            scales = tile("scales%d" % e, [P, NQ], U8)
            nc.vector.quantize_mx(out=codes[:].bitcast(FP8X4), scales=scales[:], in_=wq[:])
            nc.tensor.matmul_mx(
                out=acc[:],
                lhsT=codes[:].bitcast(FP8X4),
                lhsT_scale=scales[:],
                rhs=vw_g[:, e * DV : (e + 1) * DV].bitcast(FP8X4),
                rhs_scale=vsc_plane[:, e * DV : (e + 1) * DV],
                start=(e == order[0]),
                stop=(e == order[-1]),
            )

        unfolded = ps.tile([P, P], F32, name="unfolded", tag="score0")
        nc.tensor.transpose(unfolded[:], folded_sb[:], ident[:])
        sums_copy = tile("sums_copy", [P, P], F32)
        total = tile("total", [P, 1], F32)[:]
        nc.scalar.activation(sums_copy[:], unfolded[:], ACT.Copy, scale=inv_top, accum_out=total)
        inv_total = tile("inv_total", [P, 1], F32)[:]
        nc.vector.reciprocal(inv_total, total)
        result = tile("result", [P, DV], F32)
        nc.vector.tensor_scalar_mul(result[:], acc[:], inv_total)
        nc.sync.dma_start(out[0], result[:])
